import numpy as np
import ml_dtypes


def mxq(x, axis, fmt="e4m3"):
    dtype, down = {"e4m3": (ml_dtypes.float8_e4m3fn, 7), "e5m2": (ml_dtypes.float8_e5m2, 14)}[fmt]
    v = np.moveaxis(np.asarray(x, np.float32).astype(ml_dtypes.bfloat16).astype(np.float64), axis, -1)
    blocks = v.reshape(v.shape[:-1] + (-1, 32))
    amax = np.abs(blocks).max(-1, keepdims=True)
    byte = np.maximum(np.where(amax > 0, np.frexp(amax)[1] - 1 + 127, 0) - down, 1)
    scale = np.exp2(byte - 127.0)
    codes = (blocks / scale).astype(np.float32).astype(dtype).astype(np.float64)
    return np.moveaxis((codes * scale).reshape(v.shape), -1, axis)


WIDE = False


def mx_kscale(k):
    if not WIDE:
        return np.ones(k)
    levels = np.array([18, -18])
    if k % 512:
        return np.exp2(np.random.permutation(np.resize(levels, k // 32))).repeat(32)
    a = np.empty((k // 512, 16))
    for p in range(k // 512):
        a[p, :8] = np.random.permutation(np.resize(levels, 8))
        for g in range(8):
            far = levels[np.abs(levels - a[p, g]) >= 10]
            a[p, g + 8] = far[np.random.randint(len(far))]
    return np.exp2(a.ravel()).repeat(32)


def f64(x):
    return np.asarray(x).astype(np.float64)


def striped(idx):
    return np.tile(np.asarray(idx).reshape(-1, 16).T, (8, 1)).astype(np.uint16)


def unstriped(offs):
    return offs[:16].T.reshape(-1).astype(np.int64)


B = 2


def setup_inputs():
    n = np.random.standard_normal
    uni = np.random.uniform
    idx = np.random.permutation(2048)[:1024]
    f_f = mx_kscale(512)
    return {
        "h": (n((2, 512, 512)) * f_f[:, None]).astype(np.float32),
        "w2": (n((2, 512, 512)) / np.sqrt(512) / f_f[:, None]).astype(np.float32),
        "dyT": (n((512, 2048)) / np.sqrt(512)).astype(np.float32),
        "offs": striped(idx),
    }


def reference(h, w2, dyT, offs):
    idx = unstriped(offs).reshape(B, 512)
    dyT_i = f64(dyT)[:, idx].transpose(1, 0, 2)
    y = mxq(f64(h), 1, "e4m3").transpose(0, 2, 1) @ mxq(f64(w2), 1, "e4m3")
    dyr = dyT_i.transpose(0, 2, 1)
    s = (y * dyr).sum(-1, keepdims=True)
    out = s.transpose(0, 2, 1)
    return out

@@ -1,0 +1,114 @@
+from contextlib import ExitStack
+
+import concourse.mybir as mybir
+from concourse.masks import make_identity
+
+EXPERTS, F, E, SLOTS, TOKENS = 2, 512, 512, 512, 2048
+FLOPS = 2 * EXPERTS * SLOTS * E * (F + 1)
+
+F32 = mybir.dt.float32
+BF16 = mybir.dt.bfloat16
+U32 = mybir.dt.uint32
+U16 = mybir.dt.uint16
+U8 = mybir.dt.uint8
+FP8X4 = mybir.dt.float8_e4m3fn_x4
+MULT = mybir.AluOpType.mult
+
+P = 128
+PACK = 4
+LANES = 16
+BLOCK = 32
+E_TILES = E // P
+SLOT_TILES = SLOTS // P
+
+
+def tile_attend_gdgate_kernel(tc, h, w2, dyT, offs, out):
+    nc = tc.nc
+    with ExitStack() as ctx:
+        keep = ctx.enter_context(tc.tile_pool(name="keep", bufs=1))
+        turn_psum = ctx.enter_context(tc.psum_pool(name="turn", bufs=4))
+        y_psum = ctx.enter_context(tc.psum_pool(name="y", bufs=4))
+
+        offsets = keep.tile([P, EXPERTS * SLOTS // LANES], U16, name="offsets")
+        nc.sync.dma_start(offsets[:], offs)
+
+        windows = []
+        for et in range(E_TILES):
+            window = keep.tile([P, TOKENS], F32, name="window%d" % et)
+            nc.sync.dma_start(window[:], dyT[et * P : (et + 1) * P, :])
+            windows.append(window)
+
+        pieces = [
+            ("w", w2, 0, 0, 256, "s"), ("w", w2, 0, 256, 256, "v"),
+            ("h", h, 0, 0, 256, "v"), ("h", h, 0, 256, 256, "s"),
+            ("w", w2, 1, 0, 256, "s"), ("w", w2, 1, 256, 256, "s"),
+            ("h", h, 1, 0, 256, "s"), ("h", h, 1, 256, 128, "s"), ("h", h, 1, 384, 128, "s"),
+        ]
+        raws = []
+        for n, (name, src, b, c0, width, eng) in enumerate(pieces):
+            raw = keep.tile([P, PACK, width], F32, name="raw%d" % n)
+            nc.sync.dma_start(raw[:], src[b].rearrange("(p j) c -> p j c", j=PACK)[:, :, c0 : c0 + width])
+            raws.append(raw)
+
+        identity = keep.tile([P, P], F32, name="identity")
+        make_identity(nc, identity[:])
+        sums = keep.tile([P, BLOCK], F32, name="sums", align_bytes=64)
+        nc.gpsimd.memset(sums[:], 0.0)
+
+        grads = [keep.tile([P, SLOT_TILES, E], F32, name="grad%d" % b) for b in range(EXPERTS)]
+        cols = SLOTS // LANES
+        for et in range(E_TILES):
+            for b in range(EXPERTS):
+                picked = keep.tile([P, SLOTS], F32, name="picked%d_%d" % (et, b))
+                nc.vector.tensor_copy(picked[:], windows[et][:].indirect(offsets[:, b * cols : (b + 1) * cols]))
+                turned = turn_psum.tile([P, SLOT_TILES, P], F32, name="turned")
+                for st in range(SLOT_TILES):
+                    nc.tensor.transpose(turned[:, st, :], picked[:, st * P : (st + 1) * P], identity[:])
+                nc.scalar.copy(grads[b][:, :, et * P : (et + 1) * P], turned[:])
+
+        codes = {}
+        scales = {}
+        for name in ("w", "h"):
+            for b in range(EXPERTS):
+                codes[name, b] = keep.tile([P, SLOTS], U32, name="codes_%s%d" % (name, b), align_bytes=64)
+                scales[name, b] = keep.tile([P, SLOTS], U8, name="scales_%s%d" % (name, b), align_bytes=64)
+
+        for n, (name, src, b, c0, width, eng) in enumerate(pieces):
+            grouped = keep.tile([P, width, PACK], BF16, name="grouped%d" % n, align_bytes=64)
+            dst = grouped[:].rearrange("p (c i) t -> p c t i", i=4)
+            source = raws[n][:].rearrange("p t (c i) -> p c t i", i=4)
+            if eng == "s":
+                nc.scalar.copy(dst, source)
+            else:
+                nc.vector.tensor_copy(dst, source)
+            nc.vector.quantize_mx(
+                out=codes[name, b][:, c0 : c0 + width].bitcast(FP8X4),
+                scales=scales[name, b][:, c0 : c0 + width],
+                in_=grouped[:].rearrange("p c t -> p (c t)"),
+            )
+            if name == "h":
+                for st in range(c0 // P, (c0 + width) // P):
+                    slots = slice(st * P, (st + 1) * P)
+                    y = y_psum.tile([P, E], F32, name="y")
+                    nc.tensor.matmul_mx(
+                        out=y[:],
+                        lhsT=codes["h", b][:, slots].bitcast(FP8X4),
+                        lhsT_scale=scales["h", b][:, slots],
+                        rhs=codes["w", b][:].bitcast(FP8X4),
+                        rhs_scale=scales["w", b][:],
+                        start=True,
+                        stop=True,
+                    )
+                    col = b * SLOT_TILES + st
+                    nc.vector.scalar_tensor_tensor(
+                        out=grads[b][:, st, :], in0=y[:], scalar=1.0, in1=grads[b][:, st, :],
+                        op0=MULT, op1=MULT, accum_out=sums[:, col : col + 1],
+                    )
+
+        rows = keep.tile([P, BLOCK], F32, name="rows", align_bytes=64)
+        nc.vector.transpose(rows[:], sums[:])
+        out_rows = out.rearrange("b o (s q c) -> q (b o s) c", q=P // BLOCK, c=BLOCK)
+        tiles = EXPERTS * SLOT_TILES
+        for q in range(P // BLOCK):
+            queue = nc.sync if q % 2 == 0 else nc.scalar
+            queue.dma_start(out_rows[q], rows[q * BLOCK : q * BLOCK + tiles, :])

@@ -12,22 +12,28 @@ U32 = mybir.dt.uint32
 U16 = mybir.dt.uint16
 U8 = mybir.dt.uint8
 FP8X4 = mybir.dt.float8_e4m3fn_x4
-MULT = mybir.AluOpType.mult
 
 P = 128
 PACK = 4
 LANES = 16
 BLOCK = 32
 E_TILES = E // P
-SLOT_TILES = SLOTS // P
+HALF = 256
+HALVES = EXPERTS * SLOTS // HALF
 
 
 def tile_attend_gdgate_kernel(tc, h, w2, dyT, offs, out):
     nc = tc.nc
     with ExitStack() as ctx:
         keep = ctx.enter_context(tc.tile_pool(name="keep", bufs=1))
-        turn_psum = ctx.enter_context(tc.psum_pool(name="turn", bufs=4))
+        sum_psum = ctx.enter_context(tc.psum_pool(name="sum", bufs=1))
         y_psum = ctx.enter_context(tc.psum_pool(name="y", bufs=4))
+
+        raws = {}
+        for b in range(EXPERTS):
+            for name, src in (("h", h), ("w", w2)):
+                raws[name, b] = keep.tile([P, PACK, SLOTS], F32, name="raw_%s%d" % (name, b))
+                nc.sync.dma_start(raws[name, b][:], src[b].rearrange("(p j) c -> p j c", j=PACK))
 
         offsets = keep.tile([P, EXPERTS * SLOTS // LANES], U16, name="offsets")
         nc.sync.dma_start(offsets[:], offs)
@@ -38,77 +44,74 @@ def tile_attend_gdgate_kernel(tc, h, w2, dyT, offs, out):
             nc.sync.dma_start(window[:], dyT[et * P : (et + 1) * P, :])
             windows.append(window)
 
-        pieces = [
-            ("w", w2, 0, 0, 256, "s"), ("w", w2, 0, 256, 256, "v"),
-            ("h", h, 0, 0, 256, "v"), ("h", h, 0, 256, 256, "s"),
-            ("w", w2, 1, 0, 256, "s"), ("w", w2, 1, 256, 256, "s"),
-            ("h", h, 1, 0, 256, "s"), ("h", h, 1, 256, 128, "s"), ("h", h, 1, 384, 128, "s"),
-        ]
-        raws = []
-        for n, (name, src, b, c0, width, eng) in enumerate(pieces):
-            raw = keep.tile([P, PACK, width], F32, name="raw%d" % n)
-            nc.sync.dma_start(raw[:], src[b].rearrange("(p j) c -> p j c", j=PACK)[:, :, c0 : c0 + width])
-            raws.append(raw)
-
         identity = keep.tile([P, P], F32, name="identity")
         make_identity(nc, identity[:])
         sums = keep.tile([P, BLOCK], F32, name="sums", align_bytes=64)
         nc.gpsimd.memset(sums[:], 0.0)
 
-        grads = [keep.tile([P, SLOT_TILES, E], F32, name="grad%d" % b) for b in range(EXPERTS)]
-        cols = SLOTS // LANES
+        ys = {}
+        for b in range(EXPERTS):
+            codes = {}
+            scales = {}
+            for name in ("h", "w"):
+                codes[name] = keep.tile([P, SLOTS], U32, name="codes_%s%d" % (name, b), align_bytes=64)
+                scales[name] = keep.tile([P, SLOTS], U8, name="scales_%s%d" % (name, b), align_bytes=64)
+                for half in range(2):
+                    cols = slice(half * HALF, (half + 1) * HALF)
+                    grouped = keep.tile([P, HALF, PACK], BF16, name="grouped_%s%d_%d" % (name, b, half), align_bytes=64)
+                    dst = grouped[:].rearrange("p (c i) t -> p c t i", i=4)
+                    source = raws[name, b][:, :, cols].rearrange("p t (c i) -> p c t i", i=4)
+                    if half == 0:
+                        nc.vector.tensor_copy(dst, source)
+                    else:
+                        nc.scalar.copy(dst, source)
+                    nc.vector.quantize_mx(
+                        out=codes[name][:, cols].bitcast(FP8X4),
+                        scales=scales[name][:, cols],
+                        in_=grouped[:].rearrange("p c t -> p (c t)"),
+                    )
+            for et in range(E_TILES):
+                feats = slice(et * P, (et + 1) * P)
+                y_bank = y_psum.tile([P, SLOTS], F32, name="y_bank")
+                nc.tensor.matmul_mx(
+                    out=y_bank[:],
+                    lhsT=codes["w"][:, feats].bitcast(FP8X4),
+                    lhsT_scale=scales["w"][:, feats],
+                    rhs=codes["h"][:].bitcast(FP8X4),
+                    rhs_scale=scales["h"][:],
+                    start=True,
+                    stop=True,
+                )
+                ys[b, et] = keep.tile([P, SLOTS], F32, name="y%d_%d" % (b, et))
+                nc.scalar.copy(ys[b, et][:], y_bank[:])
+
+        banks = [sum_psum.tile([P, HALF // P, P], F32, name="sum%d" % n) for n in range(HALVES)]
         for et in range(E_TILES):
             for b in range(EXPERTS):
-                picked = keep.tile([P, SLOTS], F32, name="picked%d_%d" % (et, b))
-                nc.vector.tensor_copy(picked[:], windows[et][:].indirect(offsets[:, b * cols : (b + 1) * cols]))
-                turned = turn_psum.tile([P, SLOT_TILES, P], F32, name="turned")
-                for st in range(SLOT_TILES):
-                    nc.tensor.transpose(turned[:, st, :], picked[:, st * P : (st + 1) * P], identity[:])
-                nc.scalar.copy(grads[b][:, :, et * P : (et + 1) * P], turned[:])
-
-        codes = {}
-        scales = {}
-        for name in ("w", "h"):
-            for b in range(EXPERTS):
-                codes[name, b] = keep.tile([P, SLOTS], U32, name="codes_%s%d" % (name, b), align_bytes=64)
-                scales[name, b] = keep.tile([P, SLOTS], U8, name="scales_%s%d" % (name, b), align_bytes=64)
-
-        for n, (name, src, b, c0, width, eng) in enumerate(pieces):
-            grouped = keep.tile([P, width, PACK], BF16, name="grouped%d" % n, align_bytes=64)
-            dst = grouped[:].rearrange("p (c i) t -> p c t i", i=4)
-            source = raws[n][:].rearrange("p t (c i) -> p c t i", i=4)
-            if eng == "s":
-                nc.scalar.copy(dst, source)
-            else:
-                nc.vector.tensor_copy(dst, source)
-            nc.vector.quantize_mx(
-                out=codes[name, b][:, c0 : c0 + width].bitcast(FP8X4),
-                scales=scales[name, b][:, c0 : c0 + width],
-                in_=grouped[:].rearrange("p c t -> p (c t)"),
-            )
-            if name == "h":
-                for st in range(c0 // P, (c0 + width) // P):
-                    slots = slice(st * P, (st + 1) * P)
-                    y = y_psum.tile([P, E], F32, name="y")
-                    nc.tensor.matmul_mx(
-                        out=y[:],
-                        lhsT=codes["h", b][:, slots].bitcast(FP8X4),
-                        lhsT_scale=scales["h", b][:, slots],
-                        rhs=codes["w", b][:].bitcast(FP8X4),
-                        rhs_scale=scales["w", b][:],
-                        start=True,
-                        stop=True,
+                width = HALF if (et, b) == (E_TILES - 1, EXPERTS - 1) else SLOTS
+                for s0 in range(0, SLOTS, width):
+                    first = b * SLOTS + s0
+                    product = keep.tile([P, width], F32, name="product%d_%d" % (et, first))
+                    nc.vector.tensor_tensor(
+                        product[:],
+                        windows[et][:].indirect(offsets[:, first // LANES : (first + width) // LANES]),
+                        ys[b, et][:, s0 : s0 + width],
+                        mybir.AluOpType.mult,
                     )
-                    col = b * SLOT_TILES + st
-                    nc.vector.scalar_tensor_tensor(
-                        out=grads[b][:, st, :], in0=y[:], scalar=1.0, in1=grads[b][:, st, :],
-                        op0=MULT, op1=MULT, accum_out=sums[:, col : col + 1],
-                    )
+                    for c0 in range(0, width, P):
+                        n, st = divmod((first + c0) // P, HALF // P)
+                        nc.tensor.matmul(
+                            banks[n][:, st, :], product[:, c0 : c0 + P], identity[:],
+                            start=(et == 0 and st == 0), stop=(et == E_TILES - 1 and st == HALF // P - 1),
+                            is_transpose=True,
+                        )
+        for n in range(HALVES):
+            nc.vector.tensor_reduce(sums[:, 2 * n : 2 * n + 2], banks[n][:], mybir.AxisListType.X, mybir.AluOpType.add)
 
         rows = keep.tile([P, BLOCK], F32, name="rows", align_bytes=64)
         nc.vector.transpose(rows[:], sums[:])
         out_rows = out.rearrange("b o (s q c) -> q (b o s) c", q=P // BLOCK, c=BLOCK)
-        tiles = EXPERTS * SLOT_TILES
+        tiles = EXPERTS * SLOTS // P
         for q in range(P // BLOCK):
             queue = nc.sync if q % 2 == 0 else nc.scalar
             queue.dma_start(out_rows[q], rows[q * BLOCK : q * BLOCK + tiles, :])

@@ -19,7 +19,6 @@ LANES = 16
 BLOCK = 32
 E_TILES = E // P
 HALF = 256
-HALVES = EXPERTS * SLOTS // HALF
 
 
 def tile_attend_gdgate_kernel(tc, h, w2, dyT, offs, out):
@@ -27,86 +26,110 @@ def tile_attend_gdgate_kernel(tc, h, w2, dyT, offs, out):
     with ExitStack() as ctx:
         keep = ctx.enter_context(tc.tile_pool(name="keep", bufs=1))
         sum_psum = ctx.enter_context(tc.psum_pool(name="sum", bufs=1))
-        y_psum = ctx.enter_context(tc.psum_pool(name="y", bufs=4))
+        y_psum = ctx.enter_context(tc.psum_pool(name="y", bufs=3))
 
-        raws = {}
-        for b in range(EXPERTS):
-            for name, src in (("h", h), ("w", w2)):
-                raws[name, b] = keep.tile([P, PACK, SLOTS], F32, name="raw_%s%d" % (name, b))
-                nc.sync.dma_start(raws[name, b][:], src[b].rearrange("(p j) c -> p j c", j=PACK))
+        def load_operand(name, src, b, c0, width):
+            raw = keep.tile([P, PACK, width], F32, name="raw_%s%d_%d" % (name, b, c0))
+            nc.sync.dma_start(raw[:], src[b].rearrange("(p j) c -> p j c", j=PACK)[:, :, c0 : c0 + width])
+            return raw
 
-        offsets = keep.tile([P, EXPERTS * SLOTS // LANES], U16, name="offsets")
-        nc.sync.dma_start(offsets[:], offs)
-
-        windows = []
-        for et in range(E_TILES):
+        def load_window(et):
             window = keep.tile([P, TOKENS], F32, name="window%d" % et)
             nc.sync.dma_start(window[:], dyT[et * P : (et + 1) * P, :])
-            windows.append(window)
+            return window
+
+        raw_h0 = load_operand("h", h, 0, 0, SLOTS)
+        raw_w0 = load_operand("w", w2, 0, 0, E)
+        raw_h1 = load_operand("h", h, 1, 0, SLOTS)
+        raw_w1 = load_operand("w", w2, 1, 0, E)
+        offsets = keep.tile([P, EXPERTS * SLOTS // LANES], U16, name="offsets")
+        nc.sync.dma_start(offsets[:], offs)
+        windows = [load_window(et) for et in range(E_TILES)]
 
         identity = keep.tile([P, P], F32, name="identity")
         make_identity(nc, identity[:])
         sums = keep.tile([P, BLOCK], F32, name="sums", align_bytes=64)
         nc.gpsimd.memset(sums[:], 0.0)
 
-        ys = {}
-        for b in range(EXPERTS):
-            codes = {}
-            scales = {}
-            for name in ("h", "w"):
-                codes[name] = keep.tile([P, SLOTS], U32, name="codes_%s%d" % (name, b), align_bytes=64)
-                scales[name] = keep.tile([P, SLOTS], U8, name="scales_%s%d" % (name, b), align_bytes=64)
-                for half in range(2):
-                    cols = slice(half * HALF, (half + 1) * HALF)
-                    grouped = keep.tile([P, HALF, PACK], BF16, name="grouped_%s%d_%d" % (name, b, half), align_bytes=64)
-                    dst = grouped[:].rearrange("p (c i) t -> p c t i", i=4)
-                    source = raws[name, b][:, :, cols].rearrange("p t (c i) -> p c t i", i=4)
-                    if half == 0:
-                        nc.vector.tensor_copy(dst, source)
-                    else:
-                        nc.scalar.copy(dst, source)
-                    nc.vector.quantize_mx(
-                        out=codes[name][:, cols].bitcast(FP8X4),
-                        scales=scales[name][:, cols],
-                        in_=grouped[:].rearrange("p c t -> p (c t)"),
-                    )
-            for et in range(E_TILES):
-                feats = slice(et * P, (et + 1) * P)
+        ys = [keep.tile([P, EXPERTS * SLOTS], F32, name="y%d" % et) for et in range(E_TILES)]
+
+        def quantise(name, raw, vector_cols):
+            width = raw.shape[2]
+            grouped = keep.tile([P, width, PACK], BF16, name="grouped_" + name, align_bytes=64)
+            codes = keep.tile([P, width], U32, name="codes_" + name, align_bytes=64)
+            scales = keep.tile([P, width], U8, name="scales_" + name, align_bytes=64)
+            edges = sorted(set([0, min(HALF, vector_cols), vector_cols, width]))
+            for c0, c1 in zip(edges, edges[1:]):
+                dst = grouped[:, c0:c1, :].rearrange("p (c i) t -> p c t i", i=4)
+                source = raw[:, :, c0:c1].rearrange("p t (c i) -> p c t i", i=4)
+                if c0 < vector_cols:
+                    nc.vector.tensor_copy(dst, source)
+                else:
+                    nc.scalar.copy(dst, source)
+            for c0 in range(0, width, HALF):
+                nc.vector.quantize_mx(
+                    out=codes[:, c0 : c0 + HALF].bitcast(FP8X4),
+                    scales=scales[:, c0 : c0 + HALF],
+                    in_=grouped[:, c0 : c0 + HALF, :].rearrange("p c t -> p (c t)"),
+                )
+            return codes, scales
+
+        def expert_results(b, hidden, weights, first_et):
+            for n in range(weights[0].shape[1] // P):
+                feats = slice(n * P, (n + 1) * P)
                 y_bank = y_psum.tile([P, SLOTS], F32, name="y_bank")
                 nc.tensor.matmul_mx(
                     out=y_bank[:],
-                    lhsT=codes["w"][:, feats].bitcast(FP8X4),
-                    lhsT_scale=scales["w"][:, feats],
-                    rhs=codes["h"][:].bitcast(FP8X4),
-                    rhs_scale=scales["h"][:],
+                    lhsT=weights[0][:, feats].bitcast(FP8X4),
+                    lhsT_scale=weights[1][:, feats],
+                    rhs=hidden[0][:].bitcast(FP8X4),
+                    rhs_scale=hidden[1][:],
                     start=True,
                     stop=True,
                 )
-                ys[b, et] = keep.tile([P, SLOTS], F32, name="y%d_%d" % (b, et))
-                nc.scalar.copy(ys[b, et][:], y_bank[:])
+                nc.scalar.copy(ys[first_et + n][:, b * SLOTS : (b + 1) * SLOTS], y_bank[:])
 
-        banks = [sum_psum.tile([P, HALF // P, P], F32, name="sum%d" % n) for n in range(HALVES)]
+        h0 = quantise("h0", raw_h0, 384)
+        w0 = quantise("w0", raw_w0, 384)
+        h1 = quantise("h1", raw_h1, 384)
+        w1 = quantise("w1", raw_w1, 256)
+        expert_results(0, h0, w0, 0)
+        expert_results(1, h1, w1, 0)
+
+        last_cuts = (2 * P, 2 * P, 2 * P, P, P)
+        cuts = [(SLOTS, SLOTS), (EXPERTS * SLOTS,), (EXPERTS * SLOTS,), last_cuts]
+        banks = [sum_psum.tile([P, width // P, P], F32, name="sum%d" % n) for n, width in enumerate(last_cuts)]
+        places = [(n, st) for n, width in enumerate(last_cuts) for st in range(width // P)]
         for et in range(E_TILES):
-            for b in range(EXPERTS):
-                width = HALF if (et, b) == (E_TILES - 1, EXPERTS - 1) else SLOTS
-                for s0 in range(0, SLOTS, width):
-                    first = b * SLOTS + s0
-                    product = keep.tile([P, width], F32, name="product%d_%d" % (et, first))
-                    nc.vector.tensor_tensor(
-                        product[:],
-                        windows[et][:].indirect(offsets[:, first // LANES : (first + width) // LANES]),
-                        ys[b, et][:, s0 : s0 + width],
-                        mybir.AluOpType.mult,
+            first = 0
+            for width in cuts[et]:
+                product = keep.tile([P, width], F32, name="product%d_%d" % (et, first))
+                nc.vector.tensor_tensor(
+                    product[:],
+                    windows[et][:].indirect(offsets[:, first // LANES : (first + width) // LANES]),
+                    ys[et][:, first : first + width],
+                    mybir.AluOpType.mult,
+                )
+                for c0 in range(0, width, P):
+                    n, st = places[(first + c0) // P]
+                    nc.tensor.matmul(
+                        banks[n][:, st, :], product[:, c0 : c0 + P], identity[:],
+                        start=(et == 0 and st == 0), stop=(et == E_TILES - 1 and st == last_cuts[n] // P - 1),
+                        is_transpose=True,
                     )
-                    for c0 in range(0, width, P):
-                        n, st = divmod((first + c0) // P, HALF // P)
-                        nc.tensor.matmul(
-                            banks[n][:, st, :], product[:, c0 : c0 + P], identity[:],
-                            start=(et == 0 and st == 0), stop=(et == E_TILES - 1 and st == HALF // P - 1),
-                            is_transpose=True,
-                        )
-        for n in range(HALVES):
-            nc.vector.tensor_reduce(sums[:, 2 * n : 2 * n + 2], banks[n][:], mybir.AxisListType.X, mybir.AluOpType.add)
+                first = first + width
+        scalar_tiles = 6
+        spill = keep.tile([P, scalar_tiles, P], F32, name="spill")
+        for col, (n, st) in enumerate(places):
+            if col < scalar_tiles:
+                nc.scalar.activation(
+                    spill[:, col, :], banks[n][:, st, :], mybir.ActivationFunctionType.Copy,
+                    accum_out=sums[:, col : col + 1],
+                )
+            else:
+                nc.vector.tensor_reduce(
+                    sums[:, col : col + 1], banks[n][:, st, :], mybir.AxisListType.X, mybir.AluOpType.add
+                )
 
         rows = keep.tile([P, BLOCK], F32, name="rows", align_bytes=64)
         nc.vector.transpose(rows[:], sums[:])

@@ -118,10 +118,10 @@ def tile_attend_gdgate_kernel(tc, h, w2, dyT, offs, out):
                         is_transpose=True,
                     )
                 first = first + width
-        scalar_tiles = 6
+        scalar_tiles = 8
         spill = keep.tile([P, scalar_tiles, P], F32, name="spill")
         for col, (n, st) in enumerate(places):
-            if col < scalar_tiles:
+            if col != 6:
                 nc.scalar.activation(
                     spill[:, col, :], banks[n][:, st, :], mybir.ActivationFunctionType.Copy,
                     accum_out=sums[:, col : col + 1],

@@ -118,18 +118,21 @@ def tile_attend_gdgate_kernel(tc, h, w2, dyT, offs, out):
                         is_transpose=True,
                     )
                 first = first + width
-        scalar_tiles = 8
-        spill = keep.tile([P, scalar_tiles, P], F32, name="spill")
-        for col, (n, st) in enumerate(places):
-            if col != 6:
-                nc.scalar.activation(
-                    spill[:, col, :], banks[n][:, st, :], mybir.ActivationFunctionType.Copy,
-                    accum_out=sums[:, col : col + 1],
+        spill = keep.tile([P, len(places), P], F32, name="spill")
+        col = 0
+        for n, width in enumerate(last_cuts):
+            count = width // P
+            if n in (2, 3):
+                nc.vector.tensor_reduce(
+                    sums[:, col : col + count], banks[n][:], mybir.AxisListType.X, mybir.AluOpType.add
                 )
             else:
-                nc.vector.tensor_reduce(
-                    sums[:, col : col + 1], banks[n][:, st, :], mybir.AxisListType.X, mybir.AluOpType.add
-                )
+                for st in range(count):
+                    nc.scalar.activation(
+                        spill[:, col + st, :], banks[n][:, st, :], mybir.ActivationFunctionType.Copy,
+                        accum_out=sums[:, col + st : col + st + 1],
+                    )
+            col = col + count
 
         rows = keep.tile([P, BLOCK], F32, name="rows", align_bytes=64)
         nc.vector.transpose(rows[:], sums[:])

@@ -41,10 +41,12 @@ def tile_attend_gdgate_kernel(tc, h, w2, dyT, offs, out):
         raw_h0 = load_operand("h", h, 0, 0, SLOTS)
         raw_w0 = load_operand("w", w2, 0, 0, E)
         raw_h1 = load_operand("h", h, 1, 0, SLOTS)
-        raw_w1 = load_operand("w", w2, 1, 0, E)
+        raw_w1 = load_operand("w", w2, 1, 0, E - P)
         offsets = keep.tile([P, EXPERTS * SLOTS // LANES], U16, name="offsets")
         nc.sync.dma_start(offsets[:], offs)
-        windows = [load_window(et) for et in range(E_TILES)]
+        windows = [load_window(et) for et in range(E_TILES - 1)]
+        raw_late = load_operand("w", w2, 1, E - P, P)
+        windows.append(load_window(E_TILES - 1))
 
         identity = keep.tile([P, P], F32, name="identity")
         make_identity(nc, identity[:])
@@ -67,10 +69,11 @@ def tile_attend_gdgate_kernel(tc, h, w2, dyT, offs, out):
                 else:
                     nc.scalar.copy(dst, source)
             for c0 in range(0, width, HALF):
+                c1 = min(c0 + HALF, width)
                 nc.vector.quantize_mx(
-                    out=codes[:, c0 : c0 + HALF].bitcast(FP8X4),
-                    scales=scales[:, c0 : c0 + HALF],
-                    in_=grouped[:, c0 : c0 + HALF, :].rearrange("p c t -> p (c t)"),
+                    out=codes[:, c0:c1].bitcast(FP8X4),
+                    scales=scales[:, c0:c1],
+                    in_=grouped[:, c0:c1, :].rearrange("p c t -> p (c t)"),
                 )
             return codes, scales
 
@@ -97,13 +100,18 @@ def tile_attend_gdgate_kernel(tc, h, w2, dyT, offs, out):
         expert_results(1, h1, w1, 0)
 
         last_cuts = (2 * P, 2 * P, 2 * P, P, P)
-        cuts = [(SLOTS, SLOTS), (EXPERTS * SLOTS,), (EXPERTS * SLOTS,), last_cuts]
+        cuts = [(SLOTS, SLOTS), (EXPERTS * SLOTS,), (SLOTS, SLOTS), last_cuts]
         banks = [sum_psum.tile([P, width // P, P], F32, name="sum%d" % n) for n, width in enumerate(last_cuts)]
         places = [(n, st) for n, width in enumerate(last_cuts) for st in range(width // P)]
         for et in range(E_TILES):
             first = 0
             for width in cuts[et]:
-                product = keep.tile([P, width], F32, name="product%d_%d" % (et, first))
+                shared = (et, first) == (2, SLOTS)
+                if shared:
+                    expert_results(1, h1, quantise("late", raw_late, 0), E_TILES - 1)
+                product = keep.tile(
+                    [P, width], F32, name="grouped_late" if shared else "product%d_%d" % (et, first), align_bytes=64
+                )
                 nc.vector.tensor_tensor(
                     product[:],
                     windows[et][:].indirect(offsets[:, first // LANES : (first + width) // LANES]),

@@ -29,12 +29,12 @@ def tile_attend_gdgate_kernel(tc, h, w2, dyT, offs, out):
         y_psum = ctx.enter_context(tc.psum_pool(name="y", bufs=3))
 
         def load_operand(name, src, b, c0, width):
-            raw = keep.tile([P, PACK, width], F32, name="raw_%s%d_%d" % (name, b, c0))
+            raw = keep.tile([P, PACK, width], F32, name="raw_%s%d_%d" % (name, b, c0), align_bytes=256)
             nc.sync.dma_start(raw[:], src[b].rearrange("(p j) c -> p j c", j=PACK)[:, :, c0 : c0 + width])
             return raw
 
         def load_window(et):
-            window = keep.tile([P, TOKENS], F32, name="window%d" % et)
+            window = keep.tile([P, TOKENS], F32, name="window%d" % et, align_bytes=256)
             nc.sync.dma_start(window[:], dyT[et * P : (et + 1) * P, :])
             return window
 
@@ -110,7 +110,7 @@ def tile_attend_gdgate_kernel(tc, h, w2, dyT, offs, out):
                 if shared:
                     expert_results(1, h1, quantise("late", raw_late, 0), E_TILES - 1)
                 product = keep.tile(
-                    [P, width], F32, name="grouped_late" if shared else "product%d_%d" % (et, first), align_bytes=64
+                    [P, width], F32, name="raw_w1_%d" % (E - P) if shared else "product%d_%d" % (et, first), align_bytes=256
                 )
                 nc.vector.tensor_tensor(
                     product[:],

@@ -77,20 +77,21 @@ def tile_attend_gdgate_kernel(tc, h, w2, dyT, offs, out):
                 )
             return codes, scales
 
-        def expert_results(b, hidden, weights, first_et):
+        def expert_results(b, hidden, weights, first_et, width=SLOTS):
             for n in range(weights[0].shape[1] // P):
                 feats = slice(n * P, (n + 1) * P)
-                y_bank = y_psum.tile([P, SLOTS], F32, name="y_bank")
-                nc.tensor.matmul_mx(
-                    out=y_bank[:],
-                    lhsT=weights[0][:, feats].bitcast(FP8X4),
-                    lhsT_scale=weights[1][:, feats],
-                    rhs=hidden[0][:].bitcast(FP8X4),
-                    rhs_scale=hidden[1][:],
-                    start=True,
-                    stop=True,
-                )
-                nc.scalar.copy(ys[first_et + n][:, b * SLOTS : (b + 1) * SLOTS], y_bank[:])
+                for s0 in range(0, SLOTS, width):
+                    y_bank = y_psum.tile([P, width], F32, name="y_bank")
+                    nc.tensor.matmul_mx(
+                        out=y_bank[:],
+                        lhsT=weights[0][:, feats].bitcast(FP8X4),
+                        lhsT_scale=weights[1][:, feats],
+                        rhs=hidden[0][:, s0 : s0 + width].bitcast(FP8X4),
+                        rhs_scale=hidden[1][:, s0 : s0 + width],
+                        start=True,
+                        stop=True,
+                    )
+                    nc.scalar.copy(ys[first_et + n][:, b * SLOTS + s0 : b * SLOTS + s0 + width], y_bank[:])
 
         h0 = quantise("h0", raw_h0, 384)
         w0 = quantise("w0", raw_w0, 384)
@@ -100,7 +101,7 @@ def tile_attend_gdgate_kernel(tc, h, w2, dyT, offs, out):
         expert_results(1, h1, w1, 0)
 
         last_cuts = (2 * P, 2 * P, 2 * P, P, P)
-        cuts = [(SLOTS, SLOTS), (EXPERTS * SLOTS,), (SLOTS, SLOTS), last_cuts]
+        cuts = [(SLOTS, SLOTS), (EXPERTS * SLOTS,), (HALF, HALF, SLOTS), last_cuts]
         banks = [sum_psum.tile([P, width // P, P], F32, name="sum%d" % n) for n, width in enumerate(last_cuts)]
         places = [(n, st) for n, width in enumerate(last_cuts) for st in range(width // P)]
         for et in range(E_TILES):
@@ -108,7 +109,7 @@ def tile_attend_gdgate_kernel(tc, h, w2, dyT, offs, out):
             for width in cuts[et]:
                 shared = (et, first) == (2, SLOTS)
                 if shared:
-                    expert_results(1, h1, quantise("late", raw_late, 0), E_TILES - 1)
+                    expert_results(1, h1, quantise("late", raw_late, 0), E_TILES - 1, HALF)
                 product = keep.tile(
                     [P, width], F32, name="raw_w1_%d" % (E - P) if shared else "product%d_%d" % (et, first), align_bytes=256
                 )

@@ -55,12 +55,12 @@ def tile_attend_gdgate_kernel(tc, h, w2, dyT, offs, out):
 
         ys = [keep.tile([P, EXPERTS * SLOTS], F32, name="y%d" % et) for et in range(E_TILES)]
 
-        def quantise(name, raw, vector_cols):
+        def quantise(name, raw, vector_cols, step=HALF):
             width = raw.shape[2]
             grouped = keep.tile([P, width, PACK], BF16, name="grouped_" + name, align_bytes=64)
             codes = keep.tile([P, width], U32, name="codes_" + name, align_bytes=64)
             scales = keep.tile([P, width], U8, name="scales_" + name, align_bytes=64)
-            edges = sorted(set([0, min(HALF, vector_cols), vector_cols, width]))
+            edges = sorted(set([0, min(step, vector_cols), vector_cols, width]))
             for c0, c1 in zip(edges, edges[1:]):
                 dst = grouped[:, c0:c1, :].rearrange("p (c i) t -> p c t i", i=4)
                 source = raw[:, :, c0:c1].rearrange("p t (c i) -> p c t i", i=4)
@@ -68,8 +68,8 @@ def tile_attend_gdgate_kernel(tc, h, w2, dyT, offs, out):
                     nc.vector.tensor_copy(dst, source)
                 else:
                     nc.scalar.copy(dst, source)
-            for c0 in range(0, width, HALF):
-                c1 = min(c0 + HALF, width)
+            for c0 in range(0, width, step):
+                c1 = min(c0 + step, width)
                 nc.vector.quantize_mx(
                     out=codes[:, c0:c1].bitcast(FP8X4),
                     scales=scales[:, c0:c1],
@@ -96,12 +96,12 @@ def tile_attend_gdgate_kernel(tc, h, w2, dyT, offs, out):
         h0 = quantise("h0", raw_h0, 384)
         w0 = quantise("w0", raw_w0, 384)
         h1 = quantise("h1", raw_h1, 384)
-        w1 = quantise("w1", raw_w1, 256)
+        w1 = quantise("w1", raw_w1, 256, P)
         expert_results(0, h0, w0, 0)
         expert_results(1, h1, w1, 0)
 
         last_cuts = (2 * P, 2 * P, 2 * P, P, P)
-        cuts = [(SLOTS, SLOTS), (EXPERTS * SLOTS,), (HALF, HALF, SLOTS), last_cuts]
+        cuts = [(SLOTS, SLOTS), (EXPERTS * SLOTS,), (HALF, HALF, 3 * P, P), (HALF, HALF, P, P, P, P)]
         banks = [sum_psum.tile([P, width // P, P], F32, name="sum%d" % n) for n, width in enumerate(last_cuts)]
         places = [(n, st) for n, width in enumerate(last_cuts) for st in range(width // P)]
         for et in range(E_TILES):
@@ -110,11 +110,15 @@ def tile_attend_gdgate_kernel(tc, h, w2, dyT, offs, out):
                 shared = (et, first) == (2, SLOTS)
                 if shared:
                     expert_results(1, h1, quantise("late", raw_late, 0), E_TILES - 1, HALF)
-                product = keep.tile(
-                    [P, width], F32, name="raw_w1_%d" % (E - P) if shared else "product%d_%d" % (et, first), align_bytes=256
-                )
+                if (et, first) != (2, SLOTS + 3 * P):
+                    held = keep.tile(
+                        [P, SLOTS if shared else width], F32,
+                        name="raw_w1_%d" % (E - P) if shared else "product%d_%d" % (et, first), align_bytes=256,
+                    )
+                    held_first = first
+                product = held[:, first - held_first : first - held_first + width]
                 nc.vector.tensor_tensor(
-                    product[:],
+                    product,
                     windows[et][:].indirect(offsets[:, first // LANES : (first + width) // LANES]),
                     ys[et][:, first : first + width],
                     mybir.AluOpType.mult,

@@ -28,9 +28,9 @@ def tile_attend_gdgate_kernel(tc, h, w2, dyT, offs, out):
         sum_psum = ctx.enter_context(tc.psum_pool(name="sum", bufs=1))
         y_psum = ctx.enter_context(tc.psum_pool(name="y", bufs=3))
 
-        def load_operand(name, src, b, c0, width):
-            raw = keep.tile([P, PACK, width], F32, name="raw_%s%d_%d" % (name, b, c0), align_bytes=256)
-            nc.sync.dma_start(raw[:], src[b].rearrange("(p j) c -> p j c", j=PACK)[:, :, c0 : c0 + width])
+        def load_operand(name, src, b):
+            raw = keep.tile([P, PACK, src.shape[2]], F32, name="raw_%s%d" % (name, b), align_bytes=256)
+            nc.sync.dma_start(raw[:], src[b].rearrange("(p j) c -> p j c", j=PACK))
             return raw
 
         def load_window(et):
@@ -38,15 +38,13 @@ def tile_attend_gdgate_kernel(tc, h, w2, dyT, offs, out):
             nc.sync.dma_start(window[:], dyT[et * P : (et + 1) * P, :])
             return window
 
-        raw_h0 = load_operand("h", h, 0, 0, SLOTS)
-        raw_w0 = load_operand("w", w2, 0, 0, E)
-        raw_h1 = load_operand("h", h, 1, 0, SLOTS)
-        raw_w1 = load_operand("w", w2, 1, 0, E - P)
+        raw_h0 = load_operand("h", h, 0)
+        raw_w0 = load_operand("w", w2, 0)
+        raw_h1 = load_operand("h", h, 1)
+        raw_w1 = load_operand("w", w2, 1)
         offsets = keep.tile([P, EXPERTS * SLOTS // LANES], U16, name="offsets")
         nc.sync.dma_start(offsets[:], offs)
-        windows = [load_window(et) for et in range(E_TILES - 1)]
-        raw_late = load_operand("w", w2, 1, E - P, P)
-        windows.append(load_window(E_TILES - 1))
+        windows = [load_window(et) for et in range(E_TILES)]
 
         identity = keep.tile([P, P], F32, name="identity")
         make_identity(nc, identity[:])
@@ -68,8 +66,8 @@ def tile_attend_gdgate_kernel(tc, h, w2, dyT, offs, out):
                     nc.vector.tensor_copy(dst, source)
                 else:
                     nc.scalar.copy(dst, source)
-            for c0 in range(0, width, step):
-                c1 = min(c0 + step, width)
+            q_edges = sorted(set([0, step, HALF, width]))
+            for c0, c1 in zip(q_edges, q_edges[1:]):
                 nc.vector.quantize_mx(
                     out=codes[:, c0:c1].bitcast(FP8X4),
                     scales=scales[:, c0:c1],
@@ -77,54 +75,46 @@ def tile_attend_gdgate_kernel(tc, h, w2, dyT, offs, out):
                 )
             return codes, scales
 
-        def expert_results(b, hidden, weights, first_et, width=SLOTS):
-            for n in range(weights[0].shape[1] // P):
-                feats = slice(n * P, (n + 1) * P)
-                for s0 in range(0, SLOTS, width):
-                    y_bank = y_psum.tile([P, width], F32, name="y_bank")
-                    nc.tensor.matmul_mx(
-                        out=y_bank[:],
-                        lhsT=weights[0][:, feats].bitcast(FP8X4),
-                        lhsT_scale=weights[1][:, feats],
-                        rhs=hidden[0][:, s0 : s0 + width].bitcast(FP8X4),
-                        rhs_scale=hidden[1][:, s0 : s0 + width],
-                        start=True,
-                        stop=True,
-                    )
-                    nc.scalar.copy(ys[first_et + n][:, b * SLOTS + s0 : b * SLOTS + s0 + width], y_bank[:])
+        def product_pass(bank, weights, et, hidden):
+            feats = slice(et * P, (et + 1) * P)
+            nc.tensor.matmul_mx(
+                out=bank,
+                lhsT=weights[0][:, feats].bitcast(FP8X4), lhsT_scale=weights[1][:, feats],
+                rhs=hidden[0][:].bitcast(FP8X4), rhs_scale=hidden[1][:],
+                start=True, stop=True,
+            )
+
+        def expert_result(b, et):
+            y_bank = y_psum.tile([P, SLOTS], F32, name="y_bank")
+            product_pass(y_bank[:], weights[b], et, hidden[b])
+            nc.scalar.copy(ys[et][:, b * SLOTS : (b + 1) * SLOTS], y_bank[:])
 
         h0 = quantise("h0", raw_h0, 384)
         w0 = quantise("w0", raw_w0, 384)
         h1 = quantise("h1", raw_h1, 384)
         w1 = quantise("w1", raw_w1, 256, P)
-        expert_results(0, h0, w0, 0)
-        expert_results(1, h1, w1, 0)
+        hidden = [h0, h1]
+        weights = [w0, w1]
+        for b, et in ((0, 0), (0, 1), (1, 0), (1, 1), (0, 2), (1, 2), (0, 3), (1, 3)):
+            expert_result(b, et)
 
         last_cuts = (2 * P, 2 * P, 2 * P, P, P)
-        cuts = [(SLOTS, SLOTS), (EXPERTS * SLOTS,), (HALF, HALF, 3 * P, P), (HALF, HALF, P, P, P, P)]
+        cuts = [(SLOTS, SLOTS), (SLOTS, SLOTS), (SLOTS, 3 * P, P), (HALF, HALF, P, P, P, P)]
         banks = [sum_psum.tile([P, width // P, P], F32, name="sum%d" % n) for n, width in enumerate(last_cuts)]
         places = [(n, st) for n, width in enumerate(last_cuts) for st in range(width // P)]
         for et in range(E_TILES):
             first = 0
             for width in cuts[et]:
-                shared = (et, first) == (2, SLOTS)
-                if shared:
-                    expert_results(1, h1, quantise("late", raw_late, 0), E_TILES - 1, HALF)
-                if (et, first) != (2, SLOTS + 3 * P):
-                    held = keep.tile(
-                        [P, SLOTS if shared else width], F32,
-                        name="raw_w1_%d" % (E - P) if shared else "product%d_%d" % (et, first), align_bytes=256,
-                    )
-                    held_first = first
-                product = held[:, first - held_first : first - held_first + width]
+                product = keep.tile([P, width], F32, name="product%d_%d" % (et, first), align_bytes=256)
                 nc.vector.tensor_tensor(
-                    product,
+                    product[:],
                     windows[et][:].indirect(offsets[:, first // LANES : (first + width) // LANES]),
                     ys[et][:, first : first + width],
                     mybir.AluOpType.mult,
                 )
                 for c0 in range(0, width, P):
-                    n, st = places[(first + c0) // P]
+                    tile_nr = (first + c0) // P
+                    n, st = places[tile_nr]
                     nc.tensor.matmul(
                         banks[n][:, st, :], product[:, c0 : c0 + P], identity[:],
                         start=(et == 0 and st == 0), stop=(et == E_TILES - 1 and st == last_cuts[n] // P - 1),

@@ -26,11 +26,12 @@ def tile_attend_gdgate_kernel(tc, h, w2, dyT, offs, out):
     with ExitStack() as ctx:
         keep = ctx.enter_context(tc.tile_pool(name="keep", bufs=1))
         sum_psum = ctx.enter_context(tc.psum_pool(name="sum", bufs=1))
-        y_psum = ctx.enter_context(tc.psum_pool(name="y", bufs=3))
+        y_psum = ctx.enter_context(tc.psum_pool(name="y", bufs=4))
+        early = 1
 
-        def load_operand(name, src, b):
-            raw = keep.tile([P, PACK, src.shape[2]], F32, name="raw_%s%d" % (name, b), align_bytes=256)
-            nc.sync.dma_start(raw[:], src[b].rearrange("(p j) c -> p j c", j=PACK))
+        def load_operand(name, src, b, c0=0, width=E):
+            raw = keep.tile([P, PACK, width], F32, name="raw_%s%d" % (name, b), align_bytes=256)
+            nc.sync.dma_start(raw[:], src[b].rearrange("(p j) c -> p j c", j=PACK)[:, :, c0 : c0 + width])
             return raw
 
         def load_window(et):
@@ -40,25 +41,28 @@ def tile_attend_gdgate_kernel(tc, h, w2, dyT, offs, out):
 
         raw_h0 = load_operand("h", h, 0)
         raw_w0 = load_operand("w", w2, 0)
-        raw_h1 = load_operand("h", h, 1)
-        raw_w1 = load_operand("w", w2, 1)
         offsets = keep.tile([P, EXPERTS * SLOTS // LANES], U16, name="offsets")
         nc.sync.dma_start(offsets[:], offs)
-        windows = [load_window(et) for et in range(E_TILES)]
+        windows = [load_window(0)]
+        raw_h1 = load_operand("h", h, 1)
+        windows.extend([load_window(et) for et in range(1, early)])
+        raw_w1 = load_operand("w", w2, 1, 0, E - P)
+        windows.extend([load_window(et) for et in range(early, E_TILES - 1)])
+        raw_late = load_operand("late", w2, 1, E - P, P)
+        windows.append(load_window(E_TILES - 1))
 
         identity = keep.tile([P, P], F32, name="identity")
         make_identity(nc, identity[:])
         sums = keep.tile([P, BLOCK], F32, name="sums", align_bytes=64)
         nc.gpsimd.memset(sums[:], 0.0)
-
-        ys = [keep.tile([P, EXPERTS * SLOTS], F32, name="y%d" % et) for et in range(E_TILES)]
+        ys = [keep.tile([P, EXPERTS * SLOTS], F32, name="y%d" % et, align_bytes=256) for et in range(E_TILES)]
 
         def quantise(name, raw, vector_cols, step=HALF):
             width = raw.shape[2]
             grouped = keep.tile([P, width, PACK], BF16, name="grouped_" + name, align_bytes=64)
             codes = keep.tile([P, width], U32, name="codes_" + name, align_bytes=64)
             scales = keep.tile([P, width], U8, name="scales_" + name, align_bytes=64)
-            edges = sorted(set([0, min(step, vector_cols), vector_cols, width]))
+            edges = sorted(set(list(range(0, width, step)) + [vector_cols, width]))
             for c0, c1 in zip(edges, edges[1:]):
                 dst = grouped[:, c0:c1, :].rearrange("p (c i) t -> p c t i", i=4)
                 source = raw[:, :, c0:c1].rearrange("p t (c i) -> p c t i", i=4)
@@ -66,66 +70,100 @@ def tile_attend_gdgate_kernel(tc, h, w2, dyT, offs, out):
                     nc.vector.tensor_copy(dst, source)
                 else:
                     nc.scalar.copy(dst, source)
-            q_edges = sorted(set([0, step, HALF, width]))
-            for c0, c1 in zip(q_edges, q_edges[1:]):
+            for c0 in range(0, width, step):
                 nc.vector.quantize_mx(
-                    out=codes[:, c0:c1].bitcast(FP8X4),
-                    scales=scales[:, c0:c1],
-                    in_=grouped[:, c0:c1, :].rearrange("p c t -> p (c t)"),
+                    out=codes[:, c0 : c0 + step].bitcast(FP8X4),
+                    scales=scales[:, c0 : c0 + step],
+                    in_=grouped[:, c0 : c0 + step, :].rearrange("p c t -> p (c t)"),
                 )
             return codes, scales
 
-        def product_pass(bank, weights, et, hidden):
+        def product_pass(weights, et, hidden, s0, width):
+            y_bank = y_psum.tile([P, width], F32, name="y_bank")
             feats = slice(et * P, (et + 1) * P)
             nc.tensor.matmul_mx(
-                out=bank,
+                out=y_bank[:],
                 lhsT=weights[0][:, feats].bitcast(FP8X4), lhsT_scale=weights[1][:, feats],
-                rhs=hidden[0][:].bitcast(FP8X4), rhs_scale=hidden[1][:],
+                rhs=hidden[0][:, s0 : s0 + width].bitcast(FP8X4), rhs_scale=hidden[1][:, s0 : s0 + width],
                 start=True, stop=True,
             )
+            return y_bank
 
-        def expert_result(b, et):
-            y_bank = y_psum.tile([P, SLOTS], F32, name="y_bank")
-            product_pass(y_bank[:], weights[b], et, hidden[b])
-            nc.scalar.copy(ys[et][:, b * SLOTS : (b + 1) * SLOTS], y_bank[:])
+        bank_slots = (SLOTS, 2 * P, P, P)
+        banks = [sum_psum.tile([P, width // P, P], F32, name="sum%d" % n) for n, width in enumerate(bank_slots)]
+        places = [(n, st) for n, width in enumerate(bank_slots) for st in range(width // P)]
+
+        def turn(et, first, product, width):
+            for c0 in range(0, width, P):
+                n, st = places[(first + c0) // P]
+                nc.tensor.matmul(
+                    banks[n][:, st, :], product[:, c0 : c0 + P], identity[:],
+                    start=(et == 0 and st == 0), stop=(et == E_TILES - 1 and st == bank_slots[n] // P - 1),
+                    is_transpose=True,
+                )
+
+        def listed(et, first, width):
+            return windows[et][:].indirect(offsets[:, first // LANES : (first + width) // LANES])
+
+        def fused(et, first, width, name=None):
+            product = keep.tile([P, width], F32, name=name or "product%d_%d" % (et, first), align_bytes=256)
+            nc.vector.tensor_tensor(
+                product[:], listed(et, first, width), ys[et][:, first : first + width], mybir.AluOpType.mult
+            )
+            turn(et, first, product, width)
 
         h0 = quantise("h0", raw_h0, 384)
         w0 = quantise("w0", raw_w0, 384)
-        h1 = quantise("h1", raw_h1, 384)
-        w1 = quantise("w1", raw_w1, 256, P)
-        hidden = [h0, h1]
-        weights = [w0, w1]
-        for b, et in ((0, 0), (0, 1), (1, 0), (1, 1), (0, 2), (1, 2), (0, 3), (1, 3)):
-            expert_result(b, et)
-
-        last_cuts = (2 * P, 2 * P, 2 * P, P, P)
-        cuts = [(SLOTS, SLOTS), (SLOTS, SLOTS), (SLOTS, 3 * P, P), (HALF, HALF, P, P, P, P)]
-        banks = [sum_psum.tile([P, width // P, P], F32, name="sum%d" % n) for n, width in enumerate(last_cuts)]
-        places = [(n, st) for n, width in enumerate(last_cuts) for st in range(width // P)]
         for et in range(E_TILES):
+            nc.scalar.copy(ys[et][:, 0:SLOTS], product_pass(w0, et, h0, 0, SLOTS)[:])
+        plain = []
+        for et in range(early):
+            gathered = keep.tile([P, SLOTS], F32, name="gathered%d" % et, align_bytes=256)
+            nc.vector.tensor_copy(gathered[:], listed(et, SLOTS, SLOTS))
+            plain.append(gathered)
+            fused(et, 0, SLOTS)
+            if et == 0:
+                h1 = quantise("h1", raw_h1, 384)
+        w1 = quantise("w1", raw_w1, 256, P)
+        for et in range(early):
+            product = keep.tile([P, SLOTS], F32, name="late_product%d" % et, align_bytes=256)
+            for s0 in range(0, SLOTS, HALF):
+                cols = slice(s0, s0 + HALF)
+                y_bank = product_pass(w1, et, h1, s0, HALF)
+                nc.vector.tensor_tensor(product[:, cols], y_bank[:], plain[et][:, cols], mybir.AluOpType.mult)
+            for_turn = product
+            plain.append(for_turn)
+        for s0 in (0, HALF):
+            nc.scalar.copy(ys[early][:, SLOTS + s0 : SLOTS + s0 + HALF], product_pass(w1, early, h1, s0, HALF)[:])
+        for et in range(early + 1, E_TILES - 1):
+            nc.scalar.copy(ys[et][:, SLOTS : 2 * SLOTS], product_pass(w1, et, h1, 0, SLOTS)[:])
+        for et in range(early):
+            turn(et, SLOTS, plain[early + et], SLOTS)
+        cuts = [(SLOTS, SLOTS), (HALF, HALF, SLOTS), (SLOTS, HALF, P, P)]
+        for et in range(early, E_TILES):
             first = 0
-            for width in cuts[et]:
-                product = keep.tile([P, width], F32, name="product%d_%d" % (et, first), align_bytes=256)
-                nc.vector.tensor_tensor(
-                    product[:],
-                    windows[et][:].indirect(offsets[:, first // LANES : (first + width) // LANES]),
-                    ys[et][:, first : first + width],
-                    mybir.AluOpType.mult,
-                )
-                for c0 in range(0, width, P):
-                    tile_nr = (first + c0) // P
-                    n, st = places[tile_nr]
-                    nc.tensor.matmul(
-                        banks[n][:, st, :], product[:, c0 : c0 + P], identity[:],
-                        start=(et == 0 and st == 0), stop=(et == E_TILES - 1 and st == last_cuts[n] // P - 1),
-                        is_transpose=True,
+            for width in cuts[et - early]:
+                if (et, first) == (E_TILES - 2, SLOTS):
+                    late = quantise("late", raw_late, 0, P)
+                    for s0 in (0, HALF):
+                        nc.scalar.copy(
+                            ys[E_TILES - 1][:, SLOTS + s0 : SLOTS + s0 + HALF], product_pass(late, 0, h1, s0, HALF)[:]
+                        )
+                    warm = product_pass(late, 0, h1, 0, SLOTS)
+                    nc.tensor.matmul_mx(
+                        out=warm[:], lhsT=late[0][:].bitcast(FP8X4), lhsT_scale=late[1][:],
+                        rhs=h0[0][:].bitcast(FP8X4), rhs_scale=h0[1][:], start=True, stop=True,
                     )
+                    fused(et, first, width, "raw_late1")
+                else:
+                    fused(et, first, width)
                 first = first + width
+        last_cuts = bank_slots
         spill = keep.tile([P, len(places), P], F32, name="spill")
         col = 0
         for n, width in enumerate(last_cuts):
             count = width // P
-            if n in (2, 3):
+            if n in (1, 2):
                 nc.vector.tensor_reduce(
                     sums[:, col : col + count], banks[n][:], mybir.AxisListType.X, mybir.AluOpType.add
                 )

@@ -12,26 +12,30 @@ U32 = mybir.dt.uint32
 U16 = mybir.dt.uint16
 U8 = mybir.dt.uint8
 FP8X4 = mybir.dt.float8_e4m3fn_x4
+COPY = mybir.ActivationFunctionType.Copy
+MULT = mybir.AluOpType.mult
 
 P = 128
 PACK = 4
 LANES = 16
 BLOCK = 32
 E_TILES = E // P
+S_TILES = SLOTS // P
 HALF = 256
+CARRY = E_TILES - 1
+PIECES = (2 * P, P, P)
 
 
 def tile_attend_gdgate_kernel(tc, h, w2, dyT, offs, out):
     nc = tc.nc
     with ExitStack() as ctx:
         keep = ctx.enter_context(tc.tile_pool(name="keep", bufs=1))
-        sum_psum = ctx.enter_context(tc.psum_pool(name="sum", bufs=1))
-        y_psum = ctx.enter_context(tc.psum_pool(name="y", bufs=4))
-        early = 1
+        held_psum = ctx.enter_context(tc.psum_pool(name="held", bufs=1))
+        y_psum = ctx.enter_context(tc.psum_pool(name="y", bufs=2))
 
-        def load_operand(name, src, b, c0=0, width=E):
-            raw = keep.tile([P, PACK, width], F32, name="raw_%s%d" % (name, b), align_bytes=256)
-            nc.sync.dma_start(raw[:], src[b].rearrange("(p j) c -> p j c", j=PACK)[:, :, c0 : c0 + width])
+        def load_operand(name, src, b):
+            raw = keep.tile([P, PACK, E], F32, name="raw_%s%d" % (name, b), align_bytes=256)
+            nc.sync.dma_start(raw[:], src[b].rearrange("(p j) c -> p j c", j=PACK))
             return raw
 
         def load_window(et):
@@ -41,21 +45,18 @@ def tile_attend_gdgate_kernel(tc, h, w2, dyT, offs, out):
 
         raw_h0 = load_operand("h", h, 0)
         raw_w0 = load_operand("w", w2, 0)
+        raw_h1 = load_operand("h", h, 1)
+        raw_w1 = load_operand("w", w2, 1)
         offsets = keep.tile([P, EXPERTS * SLOTS // LANES], U16, name="offsets")
         nc.sync.dma_start(offsets[:], offs)
-        windows = [load_window(0)]
-        raw_h1 = load_operand("h", h, 1)
-        windows.extend([load_window(et) for et in range(1, early)])
-        raw_w1 = load_operand("w", w2, 1, 0, E - P)
-        windows.extend([load_window(et) for et in range(early, E_TILES - 1)])
-        raw_late = load_operand("late", w2, 1, E - P, P)
-        windows.append(load_window(E_TILES - 1))
+        windows = [load_window(et) for et in range(E_TILES)]
 
         identity = keep.tile([P, P], F32, name="identity")
         make_identity(nc, identity[:])
+        ones = keep.tile([P, P], F32, name="ones")
+        nc.gpsimd.memset(ones[:], 1.0)
         sums = keep.tile([P, BLOCK], F32, name="sums", align_bytes=64)
         nc.gpsimd.memset(sums[:], 0.0)
-        ys = [keep.tile([P, EXPERTS * SLOTS], F32, name="y%d" % et, align_bytes=256) for et in range(E_TILES)]
 
         def quantise(name, raw, vector_cols, step=HALF):
             width = raw.shape[2]
@@ -78,102 +79,73 @@ def tile_attend_gdgate_kernel(tc, h, w2, dyT, offs, out):
                 )
             return codes, scales
 
-        def product_pass(weights, et, hidden, s0, width):
-            y_bank = y_psum.tile([P, width], F32, name="y_bank")
-            feats = slice(et * P, (et + 1) * P)
+        def product_pass(stationary, tile, moving):
+            y_bank = y_psum.tile([P, E], F32, name="y_bank")
+            cols = slice(tile * P, (tile + 1) * P)
             nc.tensor.matmul_mx(
                 out=y_bank[:],
-                lhsT=weights[0][:, feats].bitcast(FP8X4), lhsT_scale=weights[1][:, feats],
-                rhs=hidden[0][:, s0 : s0 + width].bitcast(FP8X4), rhs_scale=hidden[1][:, s0 : s0 + width],
+                lhsT=stationary[0][:, cols].bitcast(FP8X4), lhsT_scale=stationary[1][:, cols],
+                rhs=moving[0][:].bitcast(FP8X4), rhs_scale=moving[1][:],
                 start=True, stop=True,
             )
             return y_bank
 
-        bank_slots = (SLOTS, 2 * P, P, P)
-        banks = [sum_psum.tile([P, width // P, P], F32, name="sum%d" % n) for n, width in enumerate(bank_slots)]
-        places = [(n, st) for n, width in enumerate(bank_slots) for st in range(width // P)]
-
-        def turn(et, first, product, width):
-            for c0 in range(0, width, P):
-                n, st = places[(first + c0) // P]
-                nc.tensor.matmul(
-                    banks[n][:, st, :], product[:, c0 : c0 + P], identity[:],
-                    start=(et == 0 and st == 0), stop=(et == E_TILES - 1 and st == bank_slots[n] // P - 1),
-                    is_transpose=True,
-                )
-
         def listed(et, first, width):
             return windows[et][:].indirect(offsets[:, first // LANES : (first + width) // LANES])
 
-        def fused(et, first, width, name=None):
-            product = keep.tile([P, width], F32, name=name or "product%d_%d" % (et, first), align_bytes=256)
-            nc.vector.tensor_tensor(
-                product[:], listed(et, first, width), ys[et][:, first : first + width], mybir.AluOpType.mult
-            )
-            turn(et, first, product, width)
+        places = [(n, st) for n, width in enumerate(PIECES) for st in range(width // P)]
+        turned = [held_psum.tile([P, width // P, 2 * P], F32, name="turned%d" % n) for n, width in enumerate(PIECES)]
+        added = [held_psum.tile([P, width // P, P], F32, name="added%d" % n) for n, width in enumerate(PIECES)]
+        for n, st in places:
+            nc.tensor.transpose(turned[n][:, st, P : 2 * P], ones[:], identity[:])
 
         h0 = quantise("h0", raw_h0, 384)
         w0 = quantise("w0", raw_w0, 384)
+        y0 = [keep.tile([P, E + PACK], F32, name="y0_%d" % st, align_bytes=256) for st in range(S_TILES)]
+        for st in range(S_TILES):
+            nc.scalar.copy(y0[st][:, 0:E], product_pass(h0, st, w0)[:])
+        h1 = quantise("h1", raw_h1, 384)
+        w1 = quantise("w1", raw_w1, 384, P)
+        y1 = [keep.tile([P, SLOTS], F32, name="y1_%d" % et, align_bytes=256) for et in range(E_TILES)]
+        spill = keep.tile([P, E_TILES, S_TILES, P + PACK], F32, name="spill")
+        scalar_spill = keep.tile([P, S_TILES, P], F32, name="scalar_spill")
+
         for et in range(E_TILES):
-            nc.scalar.copy(ys[et][:, 0:SLOTS], product_pass(w0, et, h0, 0, SLOTS)[:])
-        plain = []
-        for et in range(early):
+            last = et == E_TILES - 1
+            nc.scalar.copy(y1[et][:], product_pass(w1, et, h1)[:])
             gathered = keep.tile([P, SLOTS], F32, name="gathered%d" % et, align_bytes=256)
-            nc.vector.tensor_copy(gathered[:], listed(et, SLOTS, SLOTS))
-            plain.append(gathered)
-            fused(et, 0, SLOTS)
-            if et == 0:
-                h1 = quantise("h1", raw_h1, 384)
-        w1 = quantise("w1", raw_w1, 256, P)
-        for et in range(early):
-            product = keep.tile([P, SLOTS], F32, name="late_product%d" % et, align_bytes=256)
-            for s0 in range(0, SLOTS, HALF):
-                cols = slice(s0, s0 + HALF)
-                y_bank = product_pass(w1, et, h1, s0, HALF)
-                nc.vector.tensor_tensor(product[:, cols], y_bank[:], plain[et][:, cols], mybir.AluOpType.mult)
-            for_turn = product
-            plain.append(for_turn)
-        for s0 in (0, HALF):
-            nc.scalar.copy(ys[early][:, SLOTS + s0 : SLOTS + s0 + HALF], product_pass(w1, early, h1, s0, HALF)[:])
-        for et in range(early + 1, E_TILES - 1):
-            nc.scalar.copy(ys[et][:, SLOTS : 2 * SLOTS], product_pass(w1, et, h1, 0, SLOTS)[:])
-        for et in range(early):
-            turn(et, SLOTS, plain[early + et], SLOTS)
-        cuts = [(SLOTS, SLOTS), (HALF, HALF, SLOTS), (SLOTS, HALF, P, P)]
-        for et in range(early, E_TILES):
+            product = keep.tile([P, SLOTS], F32, name="product%d" % et, align_bytes=256)
             first = 0
-            for width in cuts[et - early]:
-                if (et, first) == (E_TILES - 2, SLOTS):
-                    late = quantise("late", raw_late, 0, P)
-                    for s0 in (0, HALF):
-                        nc.scalar.copy(
-                            ys[E_TILES - 1][:, SLOTS + s0 : SLOTS + s0 + HALF], product_pass(late, 0, h1, s0, HALF)[:]
-                        )
-                    warm = product_pass(late, 0, h1, 0, SLOTS)
-                    nc.tensor.matmul_mx(
-                        out=warm[:], lhsT=late[0][:].bitcast(FP8X4), lhsT_scale=late[1][:],
-                        rhs=h0[0][:].bitcast(FP8X4), rhs_scale=h0[1][:], start=True, stop=True,
-                    )
-                    fused(et, first, width, "raw_late1")
-                else:
-                    fused(et, first, width)
+            for width in PIECES:
+                nc.scalar.activation(gathered[:, first : first + width], listed(et, first, width), COPY)
                 first = first + width
-        last_cuts = bank_slots
-        spill = keep.tile([P, len(places), P], F32, name="spill")
-        col = 0
-        for n, width in enumerate(last_cuts):
-            count = width // P
-            if n in (1, 2):
-                nc.vector.tensor_reduce(
-                    sums[:, col : col + count], banks[n][:], mybir.AxisListType.X, mybir.AluOpType.add
+            first = 0
+            for width in PIECES if last else (SLOTS,):
+                nc.vector.tensor_tensor(
+                    product[:, first : first + width], listed(et, SLOTS + first, width),
+                    y1[et][:, first : first + width], MULT,
                 )
-            else:
-                for st in range(count):
-                    nc.scalar.activation(
-                        spill[:, col + st, :], banks[n][:, st, :], mybir.ActivationFunctionType.Copy,
-                        accum_out=sums[:, col + st : col + st + 1],
-                    )
-            col = col + count
+                first = first + width
+            for tile, (n, st) in enumerate(places):
+                nc.tensor.transpose(turned[n][:, st, 0:P], gathered[:, tile * P : (tile + 1) * P], identity[:])
+            for tile, (n, st) in enumerate(places):
+                nc.tensor.matmul(
+                    added[n][:, st, :], product[:, tile * P : (tile + 1) * P], identity[:],
+                    start=(et == 0 and st == 0), stop=(last and st == PIECES[n] // P - 1),
+                    is_transpose=True,
+                )
+            for tile, (n, st) in enumerate(places):
+                width = P + CARRY if last else P
+                nc.vector.scalar_tensor_tensor(
+                    spill[:, et, tile, 0:width], turned[n][:, st, 0:width], 1.0,
+                    y0[tile][:, et * P : et * P + width], MULT, MULT,
+                    accum_out=sums[:, tile : tile + 1] if last else y0[tile][:, E + et : E + et + 1],
+                )
+        for tile, (n, st) in enumerate(places):
+            nc.scalar.activation(
+                scalar_spill[:, tile, :], added[n][:, st, :], COPY,
+                accum_out=sums[:, S_TILES + tile : S_TILES + tile + 1],
+            )
 
         rows = keep.tile([P, BLOCK], F32, name="rows", align_bytes=64)
         nc.vector.transpose(rows[:], sums[:])

@@ -22,8 +22,8 @@ BLOCK = 32
 E_TILES = E // P
 S_TILES = SLOTS // P
 HALF = 256
-CARRY = E_TILES - 1
-PIECES = (2 * P, P, P)
+PLAIN_PIECES = (2 * P, P, P)
+FUSED_PIECES = (2 * P, 2 * P)
 
 
 def tile_attend_gdgate_kernel(tc, h, w2, dyT, offs, out):
@@ -31,7 +31,7 @@ def tile_attend_gdgate_kernel(tc, h, w2, dyT, offs, out):
     with ExitStack() as ctx:
         keep = ctx.enter_context(tc.tile_pool(name="keep", bufs=1))
         held_psum = ctx.enter_context(tc.psum_pool(name="held", bufs=1))
-        y_psum = ctx.enter_context(tc.psum_pool(name="y", bufs=2))
+        y_psum = ctx.enter_context(tc.psum_pool(name="y", bufs=3))
 
         def load_operand(name, src, b):
             raw = keep.tile([P, PACK, E], F32, name="raw_%s%d" % (name, b), align_bytes=256)
@@ -53,8 +53,6 @@ def tile_attend_gdgate_kernel(tc, h, w2, dyT, offs, out):
 
         identity = keep.tile([P, P], F32, name="identity")
         make_identity(nc, identity[:])
-        ones = keep.tile([P, P], F32, name="ones")
-        nc.gpsimd.memset(ones[:], 1.0)
         sums = keep.tile([P, BLOCK], F32, name="sums", align_bytes=64)
         nc.gpsimd.memset(sums[:], 0.0)
 
@@ -79,13 +77,13 @@ def tile_attend_gdgate_kernel(tc, h, w2, dyT, offs, out):
                 )
             return codes, scales
 
-        def product_pass(stationary, tile, moving):
-            y_bank = y_psum.tile([P, E], F32, name="y_bank")
-            cols = slice(tile * P, (tile + 1) * P)
+        def product_pass(weights, et, hidden):
+            y_bank = y_psum.tile([P, SLOTS], F32, name="y_bank")
+            cols = slice(et * P, (et + 1) * P)
             nc.tensor.matmul_mx(
                 out=y_bank[:],
-                lhsT=stationary[0][:, cols].bitcast(FP8X4), lhsT_scale=stationary[1][:, cols],
-                rhs=moving[0][:].bitcast(FP8X4), rhs_scale=moving[1][:],
+                lhsT=weights[0][:, cols].bitcast(FP8X4), lhsT_scale=weights[1][:, cols],
+                rhs=hidden[0][:].bitcast(FP8X4), rhs_scale=hidden[1][:],
                 start=True, stop=True,
             )
             return y_bank
@@ -93,59 +91,64 @@ def tile_attend_gdgate_kernel(tc, h, w2, dyT, offs, out):
         def listed(et, first, width):
             return windows[et][:].indirect(offsets[:, first // LANES : (first + width) // LANES])
 
-        places = [(n, st) for n, width in enumerate(PIECES) for st in range(width // P)]
-        turned = [held_psum.tile([P, width // P, 2 * P], F32, name="turned%d" % n) for n, width in enumerate(PIECES)]
-        added = [held_psum.tile([P, width // P, P], F32, name="added%d" % n) for n, width in enumerate(PIECES)]
-        for n, st in places:
-            nc.tensor.transpose(turned[n][:, st, P : 2 * P], ones[:], identity[:])
+        def spans(widths, first=0):
+            result = []
+            for width in widths:
+                result.append((first, width))
+                first = first + width
+            return result
+
+        bank_spans = spans(FUSED_PIECES + PLAIN_PIECES)
+        banks = [held_psum.tile([P, width // P, P], F32, name="sum%d" % n) for n, (first, width) in enumerate(bank_spans)]
+        places = [(n, st) for n, (first, width) in enumerate(bank_spans) for st in range(width // P)]
+
+        def turn(et, product, first, width):
+            for tile in range(first // P, (first + width) // P):
+                n, st = places[tile]
+                nc.tensor.matmul(
+                    banks[n][:, st, :], product[:, tile * P : (tile + 1) * P], identity[:],
+                    start=(et == 0 and st == 0), stop=(et == E_TILES - 1 and st == bank_spans[n][1] // P - 1),
+                    is_transpose=True,
+                )
 
         h0 = quantise("h0", raw_h0, 384)
         w0 = quantise("w0", raw_w0, 384)
-        y0 = [keep.tile([P, E + PACK], F32, name="y0_%d" % st, align_bytes=256) for st in range(S_TILES)]
-        for st in range(S_TILES):
-            nc.scalar.copy(y0[st][:, 0:E], product_pass(h0, st, w0)[:])
+        y0 = [keep.tile([P, SLOTS], F32, name="y0_%d" % et, align_bytes=256) for et in range(E_TILES)]
+        for et in range(E_TILES):
+            nc.scalar.copy(y0[et][:], product_pass(w0, et, h0)[:])
         h1 = quantise("h1", raw_h1, 384)
         w1 = quantise("w1", raw_w1, 384, P)
-        y1 = [keep.tile([P, SLOTS], F32, name="y1_%d" % et, align_bytes=256) for et in range(E_TILES)]
-        spill = keep.tile([P, E_TILES, S_TILES, P + PACK], F32, name="spill")
-        scalar_spill = keep.tile([P, S_TILES, P], F32, name="scalar_spill")
-
         for et in range(E_TILES):
             last = et == E_TILES - 1
-            nc.scalar.copy(y1[et][:], product_pass(w1, et, h1)[:])
+            y1_bank = product_pass(w1, et, h1)
             gathered = keep.tile([P, SLOTS], F32, name="gathered%d" % et, align_bytes=256)
-            product = keep.tile([P, SLOTS], F32, name="product%d" % et, align_bytes=256)
-            first = 0
-            for width in PIECES:
-                nc.scalar.activation(gathered[:, first : first + width], listed(et, first, width), COPY)
-                first = first + width
-            first = 0
-            for width in PIECES if last else (SLOTS,):
+            product = keep.tile([P, EXPERTS * SLOTS], F32, name="product%d" % et, align_bytes=256)
+            plain_spans = spans(PLAIN_PIECES if last else (SLOTS,))
+            for first, width in plain_spans:
+                nc.scalar.activation(gathered[:, first : first + width], listed(et, SLOTS + first, width), COPY)
+            for first, width in spans(FUSED_PIECES if last else (SLOTS,)):
+                cols = slice(first, first + width)
+                nc.vector.tensor_tensor(product[:, cols], listed(et, first, width), y0[et][:, cols], MULT)
+                turn(et, product, first, width)
+            for first, width in plain_spans:
+                cols = slice(first, first + width)
                 nc.vector.tensor_tensor(
-                    product[:, first : first + width], listed(et, SLOTS + first, width),
-                    y1[et][:, first : first + width], MULT,
+                    product[:, SLOTS + first : SLOTS + first + width], y1_bank[:, cols], gathered[:, cols], MULT
                 )
-                first = first + width
-            for tile, (n, st) in enumerate(places):
-                nc.tensor.transpose(turned[n][:, st, 0:P], gathered[:, tile * P : (tile + 1) * P], identity[:])
-            for tile, (n, st) in enumerate(places):
-                nc.tensor.matmul(
-                    added[n][:, st, :], product[:, tile * P : (tile + 1) * P], identity[:],
-                    start=(et == 0 and st == 0), stop=(last and st == PIECES[n] // P - 1),
-                    is_transpose=True,
+                turn(et, product, SLOTS + first, width)
+        spill = keep.tile([P, S_TILES + 2, P], F32, name="spill")
+        for n, (first, width) in enumerate(bank_spans):
+            col = first // P
+            if first <= SLOTS:
+                for st in range(width // P):
+                    nc.scalar.activation(
+                        spill[:, col + st, :], banks[n][:, st, :], COPY,
+                        accum_out=sums[:, col + st : col + st + 1],
+                    )
+            else:
+                nc.vector.tensor_reduce(
+                    sums[:, col : col + width // P], banks[n][:], mybir.AxisListType.X, mybir.AluOpType.add
                 )
-            for tile, (n, st) in enumerate(places):
-                width = P + CARRY if last else P
-                nc.vector.scalar_tensor_tensor(
-                    spill[:, et, tile, 0:width], turned[n][:, st, 0:width], 1.0,
-                    y0[tile][:, et * P : et * P + width], MULT, MULT,
-                    accum_out=sums[:, tile : tile + 1] if last else y0[tile][:, E + et : E + et + 1],
-                )
-        for tile, (n, st) in enumerate(places):
-            nc.scalar.activation(
-                scalar_spill[:, tile, :], added[n][:, st, :], COPY,
-                accum_out=sums[:, S_TILES + tile : S_TILES + tile + 1],
-            )
 
         rows = keep.tile([P, BLOCK], F32, name="rows", align_bytes=64)
         nc.vector.transpose(rows[:], sums[:])

@@ -123,7 +123,7 @@ def tile_attend_gdgate_kernel(tc, h, w2, dyT, offs, out):
             y1_bank = product_pass(w1, et, h1)
             gathered = keep.tile([P, SLOTS], F32, name="gathered%d" % et, align_bytes=256)
             product = keep.tile([P, EXPERTS * SLOTS], F32, name="product%d" % et, align_bytes=256)
-            plain_spans = spans(PLAIN_PIECES if last else (SLOTS,))
+            plain_spans = spans(PLAIN_PIECES if last else (3 * P, P))
             for first, width in plain_spans:
                 nc.scalar.activation(gathered[:, first : first + width], listed(et, SLOTS + first, width), COPY)
             for first, width in spans(FUSED_PIECES if last else (SLOTS,)):
@@ -136,13 +136,13 @@ def tile_attend_gdgate_kernel(tc, h, w2, dyT, offs, out):
                     product[:, SLOTS + first : SLOTS + first + width], y1_bank[:, cols], gathered[:, cols], MULT
                 )
                 turn(et, product, SLOTS + first, width)
-        spill = keep.tile([P, S_TILES + 2, P], F32, name="spill")
+        spill = keep.tile([P, S_TILES, P], F32, name="spill")
         for n, (first, width) in enumerate(bank_spans):
             col = first // P
-            if first <= SLOTS:
+            if n in (0, 2):
                 for st in range(width // P):
                     nc.scalar.activation(
-                        spill[:, col + st, :], banks[n][:, st, :], COPY,
+                        spill[:, n + st, :], banks[n][:, st, :], COPY,
                         accum_out=sums[:, col + st : col + st + 1],
                     )
             else:

@@ -31,7 +31,7 @@ def tile_attend_gdgate_kernel(tc, h, w2, dyT, offs, out):
     with ExitStack() as ctx:
         keep = ctx.enter_context(tc.tile_pool(name="keep", bufs=1))
         held_psum = ctx.enter_context(tc.psum_pool(name="held", bufs=1))
-        y_psum = ctx.enter_context(tc.psum_pool(name="y", bufs=3))
+        y_psum = ctx.enter_context(tc.psum_pool(name="y", bufs=1))
 
         def load_operand(name, src, b):
             raw = keep.tile([P, PACK, E], F32, name="raw_%s%d" % (name, b), align_bytes=256)
@@ -77,13 +77,14 @@ def tile_attend_gdgate_kernel(tc, h, w2, dyT, offs, out):
                 )
             return codes, scales
 
-        def product_pass(weights, et, hidden):
-            y_bank = y_psum.tile([P, SLOTS], F32, name="y_bank")
+        def product_pass(weights, et, hidden, bank, first=0, width=SLOTS):
+            y_bank = y_psum.tile([P, width], F32, name="y_bank%d" % bank)
             cols = slice(et * P, (et + 1) * P)
+            slots = slice(first, first + width)
             nc.tensor.matmul_mx(
                 out=y_bank[:],
                 lhsT=weights[0][:, cols].bitcast(FP8X4), lhsT_scale=weights[1][:, cols],
-                rhs=hidden[0][:].bitcast(FP8X4), rhs_scale=hidden[1][:],
+                rhs=hidden[0][:, slots].bitcast(FP8X4), rhs_scale=hidden[1][:, slots],
                 start=True, stop=True,
             )
             return y_bank
@@ -111,30 +112,36 @@ def tile_attend_gdgate_kernel(tc, h, w2, dyT, offs, out):
                     is_transpose=True,
                 )
 
-        h0 = quantise("h0", raw_h0, 384)
-        w0 = quantise("w0", raw_w0, 384)
+        h0 = quantise("h0", raw_h0, 256)
+        w0 = quantise("w0", raw_w0, 256)
         y0 = [keep.tile([P, SLOTS], F32, name="y0_%d" % et, align_bytes=256) for et in range(E_TILES)]
         for et in range(E_TILES):
-            nc.scalar.copy(y0[et][:], product_pass(w0, et, h0)[:])
-        h1 = quantise("h1", raw_h1, 384)
-        w1 = quantise("w1", raw_w1, 384, P)
+            nc.scalar.copy(y0[et][:], product_pass(w0, et, h0, et % 3)[:])
+        h1 = quantise("h1", raw_h1, 512)
+        w1 = quantise("w1", raw_w1, 256, P)
+        y1_banks = {0: product_pass(w1, 0, h1, 1)}
+        y1_halves = [product_pass(w1, 1, h1, 2, 0, HALF), product_pass(w1, 1, h1, 0, HALF, HALF)]
         for et in range(E_TILES):
             last = et == E_TILES - 1
-            y1_bank = product_pass(w1, et, h1)
             gathered = keep.tile([P, SLOTS], F32, name="gathered%d" % et, align_bytes=256)
             product = keep.tile([P, EXPERTS * SLOTS], F32, name="product%d" % et, align_bytes=256)
-            plain_spans = spans(PLAIN_PIECES if last else (3 * P, P))
+            plain_spans = spans(PLAIN_PIECES if last else (HALF, HALF) if et == 1 else (3 * P, P))
             for first, width in plain_spans:
                 nc.scalar.activation(gathered[:, first : first + width], listed(et, SLOTS + first, width), COPY)
             for first, width in spans(FUSED_PIECES if last else (SLOTS,)):
                 cols = slice(first, first + width)
                 nc.vector.tensor_tensor(product[:, cols], listed(et, first, width), y0[et][:, cols], MULT)
                 turn(et, product, first, width)
-            for first, width in plain_spans:
+            for n, (first, width) in enumerate(plain_spans):
                 cols = slice(first, first + width)
-                nc.vector.tensor_tensor(
-                    product[:, SLOTS + first : SLOTS + first + width], y1_bank[:, cols], gathered[:, cols], MULT
-                )
+                y = y1_halves[n][:] if et == 1 else y1_banks[et][:, cols]
+                nc.vector.tensor_tensor(product[:, SLOTS + first : SLOTS + first + width], y, gathered[:, cols], MULT)
+                if (et, n) == (1, 0):
+                    y1_banks[2] = product_pass(w1, 2, h1, 2)
+                if (et, n) == (1, 1):
+                    y1_banks[3] = product_pass(w1, 3, h1, 0)
+                if (et, n) == (2, 1):
+                    product_pass(w1, 3, h1, 2)
                 turn(et, product, SLOTS + first, width)
         spill = keep.tile([P, S_TILES, P], F32, name="spill")
         for n, (first, width) in enumerate(bank_spans):

@@ -146,10 +146,10 @@ def tile_attend_gdgate_kernel(tc, h, w2, dyT, offs, out):
         spill = keep.tile([P, S_TILES, P], F32, name="spill")
         for n, (first, width) in enumerate(bank_spans):
             col = first // P
-            if n in (0, 2):
+            if n in (0, 3, 4):
                 for st in range(width // P):
                     nc.scalar.activation(
-                        spill[:, n + st, :], banks[n][:, st, :], COPY,
+                        spill[:, max(n - 1, 0) + st, :], banks[n][:, st, :], COPY,
                         accum_out=sums[:, col + st : col + st + 1],
                     )
             else:

@@ -140,8 +140,6 @@ def tile_attend_gdgate_kernel(tc, h, w2, dyT, offs, out):
                     y1_banks[2] = product_pass(w1, 2, h1, 2)
                 if (et, n) == (1, 1):
                     y1_banks[3] = product_pass(w1, 3, h1, 0)
-                if (et, n) == (2, 1):
-                    product_pass(w1, 3, h1, 2)
                 turn(et, product, SLOTS + first, width)
         spill = keep.tile([P, S_TILES, P], F32, name="spill")
         for n, (first, width) in enumerate(bank_spans):

@@ -114,8 +114,8 @@ def tile_attend_gdgate_kernel(tc, h, w2, dyT, offs, out):
 
         h0 = quantise("h0", raw_h0, 256)
         w0 = quantise("w0", raw_w0, 256)
-        y0 = [keep.tile([P, SLOTS], F32, name="y0_%d" % et, align_bytes=256) for et in range(E_TILES)]
-        for et in range(E_TILES):
+        y0 = [keep.tile([P, SLOTS], F32, name="y0_%d" % et, align_bytes=256) for et in range(E_TILES - 1)]
+        for et in range(E_TILES - 1):
             nc.scalar.copy(y0[et][:], product_pass(w0, et, h0, et % 3)[:])
         h1 = quantise("h1", raw_h1, 512)
         w1 = quantise("w1", raw_w1, 256, P)
@@ -132,10 +132,15 @@ def tile_attend_gdgate_kernel(tc, h, w2, dyT, offs, out):
                 cols = slice(first, first + width)
                 nc.vector.tensor_tensor(product[:, cols], listed(et, first, width), y0[et][:, cols], MULT)
                 turn(et, product, first, width)
+            if et == 1:
+                y0.append(keep.tile([P, SLOTS], F32, name="y0_1", align_bytes=256))
+                nc.scalar.copy(y0[3][:], y0_last_bank[:])
             for n, (first, width) in enumerate(plain_spans):
                 cols = slice(first, first + width)
                 y = y1_halves[n][:] if et == 1 else y1_banks[et][:, cols]
                 nc.vector.tensor_tensor(product[:, SLOTS + first : SLOTS + first + width], y, gathered[:, cols], MULT)
+                if (et, n) == (0, 1):
+                    y0_last_bank = product_pass(w0, 3, h0, 1)
                 if (et, n) == (1, 0):
                     y1_banks[2] = product_pass(w1, 2, h1, 2)
                 if (et, n) == (1, 1):

@@ -22,7 +22,7 @@ BLOCK = 32
 E_TILES = E // P
 S_TILES = SLOTS // P
 HALF = 256
-PLAIN_PIECES = (2 * P, P, P)
+SUM_BANKS = (2 * P, 2 * P, 2 * P, P, P)
 FUSED_PIECES = (2 * P, 2 * P)
 
 
@@ -55,6 +55,8 @@ def tile_attend_gdgate_kernel(tc, h, w2, dyT, offs, out):
         make_identity(nc, identity[:])
         sums = keep.tile([P, BLOCK], F32, name="sums", align_bytes=64)
         nc.gpsimd.memset(sums[:], 0.0)
+        sums0 = keep.tile([P, P], F32, name="sums0", align_bytes=64)
+        nc.gpsimd.memset(sums0[:], 0.0)
 
         def quantise(name, raw, vector_cols, step=HALF):
             width = raw.shape[2]
@@ -99,7 +101,7 @@ def tile_attend_gdgate_kernel(tc, h, w2, dyT, offs, out):
                 first = first + width
             return result
 
-        bank_spans = spans(FUSED_PIECES + PLAIN_PIECES)
+        bank_spans = spans(SUM_BANKS)
         banks = [held_psum.tile([P, width // P, P], F32, name="sum%d" % n) for n, (first, width) in enumerate(bank_spans)]
         places = [(n, st) for n, (first, width) in enumerate(bank_spans) for st in range(width // P)]
 
@@ -125,7 +127,7 @@ def tile_attend_gdgate_kernel(tc, h, w2, dyT, offs, out):
             last = et == E_TILES - 1
             gathered = keep.tile([P, SLOTS], F32, name="gathered%d" % et, align_bytes=256)
             product = keep.tile([P, EXPERTS * SLOTS], F32, name="product%d" % et, align_bytes=256)
-            plain_spans = spans(PLAIN_PIECES if last else (HALF, HALF) if et == 1 else (3 * P, P))
+            plain_spans = spans((HALF, HALF))
             for first, width in plain_spans:
                 nc.scalar.activation(gathered[:, first : first + width], listed(et, SLOTS + first, width), COPY)
             for first, width in spans(FUSED_PIECES if last else (SLOTS,)):
@@ -138,7 +140,11 @@ def tile_attend_gdgate_kernel(tc, h, w2, dyT, offs, out):
             for n, (first, width) in enumerate(plain_spans):
                 cols = slice(first, first + width)
                 y = y1_halves[n][:] if et == 1 else y1_banks[et][:, cols]
-                nc.vector.tensor_tensor(product[:, SLOTS + first : SLOTS + first + width], y, gathered[:, cols], MULT)
+                dealt = product[:, SLOTS + first : SLOTS + first + width].rearrange("p (u q c) -> p q u c", u=2, c=BLOCK)
+                nc.vector.tensor_tensor(
+                    dealt, y.rearrange("p (q u c) -> p q u c", u=2, c=BLOCK),
+                    gathered[:, cols].rearrange("p (q u c) -> p q u c", u=2, c=BLOCK), MULT,
+                )
                 if (et, n) == (0, 1):
                     y0_last_bank = product_pass(w0, 3, h0, 1)
                 if (et, n) == (1, 0):
@@ -147,23 +153,22 @@ def tile_attend_gdgate_kernel(tc, h, w2, dyT, offs, out):
                     y1_banks[3] = product_pass(w1, 3, h1, 0)
                 turn(et, product, SLOTS + first, width)
         spill = keep.tile([P, S_TILES, P], F32, name="spill")
-        for n, (first, width) in enumerate(bank_spans):
-            col = first // P
-            if n in (0, 3, 4):
-                for st in range(width // P):
-                    nc.scalar.activation(
-                        spill[:, max(n - 1, 0) + st, :], banks[n][:, st, :], COPY,
-                        accum_out=sums[:, col + st : col + st + 1],
-                    )
-            else:
-                nc.vector.tensor_reduce(
-                    sums[:, col : col + width // P], banks[n][:], mybir.AxisListType.X, mybir.AluOpType.add
-                )
+        add = mybir.AluOpType.add
+        for st in range(2):
+            nc.scalar.activation(spill[:, st, :], banks[0][:, st, :], COPY, accum_out=sums0[:, st : st + 1])
+        nc.vector.tensor_reduce(sums0[:, 2:4], banks[1][:], mybir.AxisListType.X, add)
+        nc.vector.tensor_reduce(sums[:, 0:BLOCK:LANES], banks[2][:], mybir.AxisListType.X, add)
+        for u in range(2):
+            col = 8 + u * LANES
+            nc.scalar.activation(spill[:, 2 + u, :], banks[3 + u][:, 0, :], COPY, accum_out=sums[:, col : col + 1])
 
+        turned = y_psum.tile([P, P], F32, name="y_bank1")
+        nc.tensor.matmul(turned[:], sums0[:], identity[:], start=True, stop=True, is_transpose=True)
+        rows0 = keep.tile([P, P], F32, name="rows0", align_bytes=64)
+        nc.vector.tensor_copy(rows0[0:BLOCK, :], turned[0:BLOCK, :])
+        nc.sync.dma_start(out[0].rearrange("o (s c) -> (o s) c", c=P), rows0[0:S_TILES, :])
         rows = keep.tile([P, BLOCK], F32, name="rows", align_bytes=64)
         nc.vector.transpose(rows[:], sums[:])
-        out_rows = out.rearrange("b o (s q c) -> q (b o s) c", q=P // BLOCK, c=BLOCK)
-        tiles = EXPERTS * SLOTS // P
-        for q in range(P // BLOCK):
-            queue = nc.sync if q % 2 == 0 else nc.scalar
-            queue.dma_start(out_rows[q], rows[q * BLOCK : q * BLOCK + tiles, :])
+        out_runs = out[1].rearrange("o (pair m c) -> pair (o m) c", pair=2, c=BLOCK)
+        nc.scalar.dma_start(out_runs[0], rows[0:P:LANES, :])
+        nc.sync.dma_start(out_runs[1], rows[8:P:LANES, :])

@@ -55,7 +55,7 @@ def tile_attend_gdgate_kernel(tc, h, w2, dyT, offs, out):
         make_identity(nc, identity[:])
         sums = keep.tile([P, BLOCK], F32, name="sums", align_bytes=64)
         nc.gpsimd.memset(sums[:], 0.0)
-        sums0 = keep.tile([P, P], F32, name="sums0", align_bytes=64)
+        sums0 = keep.tile([P, BLOCK], F32, name="sums0", align_bytes=64)
         nc.gpsimd.memset(sums0[:], 0.0)
 
         def quantise(name, raw, vector_cols, step=HALF):
@@ -162,11 +162,12 @@ def tile_attend_gdgate_kernel(tc, h, w2, dyT, offs, out):
             col = 8 + u * LANES
             nc.scalar.activation(spill[:, 2 + u, :], banks[3 + u][:, 0, :], COPY, accum_out=sums[:, col : col + 1])
 
-        turned = y_psum.tile([P, P], F32, name="y_bank1")
-        nc.tensor.matmul(turned[:], sums0[:], identity[:], start=True, stop=True, is_transpose=True)
-        rows0 = keep.tile([P, P], F32, name="rows0", align_bytes=64)
-        nc.vector.tensor_copy(rows0[0:BLOCK, :], turned[0:BLOCK, :])
-        nc.sync.dma_start(out[0].rearrange("o (s c) -> (o s) c", c=P), rows0[0:S_TILES, :])
+        rows0 = keep.tile([P, BLOCK], F32, name="rows0", align_bytes=64)
+        nc.vector.transpose(rows0[:], sums0[:])
+        out_rows = out[0].rearrange("o (s q c) -> q (o s) c", q=P // BLOCK, c=BLOCK)
+        for q in range(P // BLOCK):
+            queue = nc.sync if q % 2 == 0 else nc.scalar
+            queue.dma_start(out_rows[q], rows0[q * BLOCK : q * BLOCK + S_TILES, :])
         rows = keep.tile([P, BLOCK], F32, name="rows", align_bytes=64)
         nc.vector.transpose(rows[:], sums[:])
         out_runs = out[1].rearrange("o (pair m c) -> pair (o m) c", pair=2, c=BLOCK)

from contextlib import ExitStack

import concourse.mybir as mybir
from concourse.masks import make_identity

EXPERTS, F, E, SLOTS, TOKENS = 2, 512, 512, 512, 2048
FLOPS = 2 * EXPERTS * SLOTS * E * (F + 1)

F32 = mybir.dt.float32
BF16 = mybir.dt.bfloat16
U32 = mybir.dt.uint32
U16 = mybir.dt.uint16
U8 = mybir.dt.uint8
FP8X4 = mybir.dt.float8_e4m3fn_x4
COPY = mybir.ActivationFunctionType.Copy
MULT = mybir.AluOpType.mult

P = 128
PACK = 4
LANES = 16
BLOCK = 32
E_TILES = E // P
S_TILES = SLOTS // P
HALF = 256
SUM_BANKS = (2 * P, 2 * P, 2 * P, P, P)
FUSED_PIECES = (2 * P, 2 * P)


def tile_attend_gdgate_kernel(tc, h, w2, dyT, offs, out):
    nc = tc.nc
    with ExitStack() as ctx:
        keep = ctx.enter_context(tc.tile_pool(name="keep", bufs=1))
        held_psum = ctx.enter_context(tc.psum_pool(name="held", bufs=1))
        y_psum = ctx.enter_context(tc.psum_pool(name="y", bufs=1))

        def load_operand(name, src, b):
            raw = keep.tile([P, PACK, E], F32, name="raw_%s%d" % (name, b), align_bytes=256)
            nc.sync.dma_start(raw[:], src[b].rearrange("(p j) c -> p j c", j=PACK))
            return raw

        def load_window(et):
            window = keep.tile([P, TOKENS], F32, name="window%d" % et, align_bytes=256)
            nc.sync.dma_start(window[:], dyT[et * P : (et + 1) * P, :])
            return window

        raw_h0 = load_operand("h", h, 0)
        raw_w0 = load_operand("w", w2, 0)
        raw_h1 = load_operand("h", h, 1)
        raw_w1 = load_operand("w", w2, 1)
        offsets = keep.tile([P, EXPERTS * SLOTS // LANES], U16, name="offsets")
        nc.sync.dma_start(offsets[:], offs)
        windows = [load_window(et) for et in range(E_TILES)]

        identity = keep.tile([P, P], F32, name="identity")
        make_identity(nc, identity[:])
        sums = keep.tile([P, BLOCK], F32, name="sums", align_bytes=64)
        nc.gpsimd.memset(sums[:], 0.0)
        sums0 = keep.tile([P, BLOCK], F32, name="sums0", align_bytes=64)
        nc.gpsimd.memset(sums0[:], 0.0)

        def quantise(name, raw, vector_cols, step=HALF):
            width = raw.shape[2]
            grouped = keep.tile([P, width, PACK], BF16, name="grouped_" + name, align_bytes=64)
            codes = keep.tile([P, width], U32, name="codes_" + name, align_bytes=64)
            scales = keep.tile([P, width], U8, name="scales_" + name, align_bytes=64)
            edges = sorted(set(list(range(0, width, step)) + [vector_cols, width]))
            for c0, c1 in zip(edges, edges[1:]):
                dst = grouped[:, c0:c1, :].rearrange("p (c i) t -> p c t i", i=4)
                source = raw[:, :, c0:c1].rearrange("p t (c i) -> p c t i", i=4)
                if c0 < vector_cols:
                    nc.vector.tensor_copy(dst, source)
                else:
                    nc.scalar.copy(dst, source)
            for c0 in range(0, width, step):
                nc.vector.quantize_mx(
                    out=codes[:, c0 : c0 + step].bitcast(FP8X4),
                    scales=scales[:, c0 : c0 + step],
                    in_=grouped[:, c0 : c0 + step, :].rearrange("p c t -> p (c t)"),
                )
            return codes, scales

        def product_pass(weights, et, hidden, bank, first=0, width=SLOTS):
            y_bank = y_psum.tile([P, width], F32, name="y_bank%d" % bank)
            cols = slice(et * P, (et + 1) * P)
            slots = slice(first, first + width)
            nc.tensor.matmul_mx(
                out=y_bank[:],
                lhsT=weights[0][:, cols].bitcast(FP8X4), lhsT_scale=weights[1][:, cols],
                rhs=hidden[0][:, slots].bitcast(FP8X4), rhs_scale=hidden[1][:, slots],
                start=True, stop=True,
            )
            return y_bank

        def listed(et, first, width):
            return windows[et][:].indirect(offsets[:, first // LANES : (first + width) // LANES])

        def spans(widths, first=0):
            result = []
            for width in widths:
                result.append((first, width))
                first = first + width
            return result

        bank_spans = spans(SUM_BANKS)
        banks = [held_psum.tile([P, width // P, P], F32, name="sum%d" % n) for n, (first, width) in enumerate(bank_spans)]
        places = [(n, st) for n, (first, width) in enumerate(bank_spans) for st in range(width // P)]

        def turn(et, product, first, width):
            for tile in range(first // P, (first + width) // P):
                n, st = places[tile]
                nc.tensor.matmul(
                    banks[n][:, st, :], product[:, tile * P : (tile + 1) * P], identity[:],
                    start=(et == 0 and st == 0), stop=(et == E_TILES - 1 and st == bank_spans[n][1] // P - 1),
                    is_transpose=True,
                )

        h0 = quantise("h0", raw_h0, 256)
        w0 = quantise("w0", raw_w0, 256)
        y0 = [keep.tile([P, SLOTS], F32, name="y0_%d" % et, align_bytes=256) for et in range(E_TILES - 1)]
        for et in range(E_TILES - 1):
            nc.scalar.copy(y0[et][:], product_pass(w0, et, h0, et % 3)[:])
        h1 = quantise("h1", raw_h1, 512)
        w1 = quantise("w1", raw_w1, 256, P)
        y1_banks = {0: product_pass(w1, 0, h1, 1)}
        y1_halves = [product_pass(w1, 1, h1, 2, 0, HALF), product_pass(w1, 1, h1, 0, HALF, HALF)]
        for et in range(E_TILES):
            last = et == E_TILES - 1
            gathered = keep.tile([P, SLOTS], F32, name="gathered%d" % et, align_bytes=256)
            product = keep.tile([P, EXPERTS * SLOTS], F32, name="product%d" % et, align_bytes=256)
            plain_spans = spans((HALF, HALF))
            for first, width in plain_spans:
                nc.scalar.activation(gathered[:, first : first + width], listed(et, SLOTS + first, width), COPY)
            for first, width in spans(FUSED_PIECES if last else (SLOTS,)):
                cols = slice(first, first + width)
                nc.vector.tensor_tensor(product[:, cols], listed(et, first, width), y0[et][:, cols], MULT)
                turn(et, product, first, width)
            if et == 1:
                y0.append(keep.tile([P, SLOTS], F32, name="y0_1", align_bytes=256))
                nc.scalar.copy(y0[3][:], y0_last_bank[:])
            for n, (first, width) in enumerate(plain_spans):
                cols = slice(first, first + width)
                y = y1_halves[n][:] if et == 1 else y1_banks[et][:, cols]
                dealt = product[:, SLOTS + first : SLOTS + first + width].rearrange("p (u q c) -> p q u c", u=2, c=BLOCK)
                nc.vector.tensor_tensor(
                    dealt, y.rearrange("p (q u c) -> p q u c", u=2, c=BLOCK),
                    gathered[:, cols].rearrange("p (q u c) -> p q u c", u=2, c=BLOCK), MULT,
                )
                if (et, n) == (0, 1):
                    y0_last_bank = product_pass(w0, 3, h0, 1)
                if (et, n) == (1, 0):
                    y1_banks[2] = product_pass(w1, 2, h1, 2)
                if (et, n) == (1, 1):
                    y1_banks[3] = product_pass(w1, 3, h1, 0)
                turn(et, product, SLOTS + first, width)
        spill = keep.tile([P, S_TILES, P], F32, name="spill")
        add = mybir.AluOpType.add
        for st in range(2):
            nc.scalar.activation(spill[:, st, :], banks[0][:, st, :], COPY, accum_out=sums0[:, st : st + 1])
        nc.vector.tensor_reduce(sums0[:, 2:4], banks[1][:], mybir.AxisListType.X, add)
        nc.vector.tensor_reduce(sums[:, 0:BLOCK:LANES], banks[2][:], mybir.AxisListType.X, add)
        for u in range(2):
            col = 8 + u * LANES
            nc.scalar.activation(spill[:, 2 + u, :], banks[3 + u][:, 0, :], COPY, accum_out=sums[:, col : col + 1])

        rows0 = keep.tile([P, BLOCK], F32, name="rows0", align_bytes=64)
        nc.vector.transpose(rows0[:], sums0[:])
        out_rows = out[0].rearrange("o (s q c) -> q (o s) c", q=P // BLOCK, c=BLOCK)
        for q in range(P // BLOCK):
            queue = nc.sync if q % 2 == 0 else nc.scalar
            queue.dma_start(out_rows[q], rows0[q * BLOCK : q * BLOCK + S_TILES, :])
        rows = keep.tile([P, BLOCK], F32, name="rows", align_bytes=64)
        nc.vector.transpose(rows[:], sums[:])
        out_runs = out[1].rearrange("o (pair m c) -> pair (o m) c", pair=2, c=BLOCK)
        nc.scalar.dma_start(out_runs[0], rows[0:P:LANES, :])
        nc.sync.dma_start(out_runs[1], rows[8:P:LANES, :])
